import numpy as np
import ml_dtypes


def mxq(x, axis, fmt="e4m3"):
    dtype, down = {"e4m3": (ml_dtypes.float8_e4m3fn, 7), "e5m2": (ml_dtypes.float8_e5m2, 14)}[fmt]
    v = np.moveaxis(np.asarray(x, np.float32).astype(ml_dtypes.bfloat16).astype(np.float64), axis, -1)
    blocks = v.reshape(v.shape[:-1] + (-1, 32))
    amax = np.abs(blocks).max(-1, keepdims=True)
    byte = np.maximum(np.where(amax > 0, np.frexp(amax)[1] - 1 + 127, 0) - down, 1)
    scale = np.exp2(byte - 127.0)
    codes = (blocks / scale).astype(np.float32).astype(dtype).astype(np.float64)
    return np.moveaxis((codes * scale).reshape(v.shape), -1, axis)


WIDE = False


def mx_kscale(k):
    if not WIDE:
        return np.ones(k)
    levels = np.array([10, -10, 5, -5, 0])
    if k % 512:
        return np.exp2(np.random.permutation(np.resize(levels, k // 32))).repeat(32)
    a = np.empty((k // 512, 16))
    for p in range(k // 512):
        a[p, :8] = np.random.permutation(np.resize(levels, 8))
        for g in range(8):
            far = levels[np.abs(levels - a[p, g]) >= 10]
            a[p, g + 8] = far[np.random.randint(len(far))]
    return np.exp2(a.ravel()).repeat(32)


def f64(x):
    return np.asarray(x).astype(np.float64)


def striped(idx):
    return np.tile(idx.reshape(-1, 16).T, (8, 1)).astype(np.uint16)


def unstriped(offs):
    return offs[:16].T.reshape(-1).astype(np.int64)


E2M1 = np.array([0.0, 0.5, 1.0, 1.5, 2.0, 3.0, 4.0, 6.0, -0.0, -0.5, -1.0, -1.5, -2.0, -3.0, -4.0, -6.0])


def pack_fp4(w):
    k, n = w.shape
    w = f64(np.asarray(w, np.float32).astype(ml_dtypes.bfloat16)).reshape(k // 32, 32, n)
    amax = np.abs(w).max(1)
    mant, ex = np.frexp(amax / 6.0)
    byte = np.clip(np.where(amax > 0, np.where(mant > 0.5, ex, ex - 1) + 127, 1), 1, 254)
    scaled = (w * np.exp2(127.0 - byte)[:, None, :]).reshape(k, n).astype(np.float32)
    c = np.ascontiguousarray(scaled.reshape(k // 512, 128, 4, n).transpose(0, 1, 3, 2)).astype(ml_dtypes.float4_e2m1fn).view(np.uint8) & 0xF
    words = (c[..., 0::2] | (c[..., 1::2] << 4)).reshape(k // 512, 128, 2 * n)
    return np.ascontiguousarray(words), np.ascontiguousarray(byte.astype(np.uint8).reshape(k // 512, 16, n))


def unpack_fp4(words, scales):
    g, _, n = scales.shape
    words = np.ascontiguousarray(words).reshape(g, 128, n, 2)
    nib = np.empty((g, 128, n, 4), np.uint8)
    nib[..., 0::2] = words & 0xF
    nib[..., 1::2] = words >> 4
    vals = E2M1[nib] * np.repeat(np.exp2(scales.astype(np.float64) - 127.0), 8, axis=1)[..., None]
    return vals.transpose(0, 1, 3, 2).reshape(g * 512, n)


def planes(y):
    n, m = y.shape
    v = y.astype(np.float32).astype(ml_dtypes.bfloat16).astype(np.float64).reshape(n // 32, 32, m)
    top = np.abs(v).max(1)
    byte = np.clip(np.where(top > 0, np.frexp(top)[1] - 1 + 127 - 7, 1), 1, 254)
    codes = (v * np.exp2(127.0 - byte)[:, None, :]).reshape(n, m).astype(np.float32).astype(ml_dtypes.float8_e4m3fn).view(np.uint8)
    words = codes.reshape(n // 512, 128, 4, m).transpose(0, 1, 3, 2)
    return np.ascontiguousarray(words), np.ascontiguousarray(byte.astype(np.uint8).reshape(n // 512, 16, m))


K, T, N, U = 512, 512, 512, 1024
P = 2 ** 7


def setup_inputs():
    n = np.random.standard_normal
    s = mx_kscale(K)[:, None]
    packed_xT = pack_fp4(n((K, T)) * s)
    return {
        "x_words": packed_xT[0],
        "x_scales": packed_xT[1],
        "gate": np.tile(np.random.uniform(0.5, 1.5, T), (P, 1)).astype(np.float32),
        "w1": (n((K, N)) / np.sqrt(K) / s).astype(np.float32),
        "dst": striped(np.random.permutation(U)[:T]),
    }


def reference(x_words, x_scales, gate, w1, dst):
    xq = unpack_fp4(x_words, x_scales)
    y = mxq(f64(w1), 0, "e4m3").T @ xq
    out = np.zeros((N, U))
    out[:, unstriped(dst)] = y * f64(gate)[:1]
    return (out,) + planes(out)

@@ -1,0 +1,135 @@
+from contextlib import ExitStack
+
+import concourse.mybir as mybir
+
+F32 = mybir.dt.float32
+BF16 = mybir.dt.bfloat16
+I32 = mybir.dt.int32
+U32 = mybir.dt.uint32
+U16 = mybir.dt.uint16
+U8 = mybir.dt.uint8
+FP8X4 = mybir.dt.float8_e4m3fn_x4
+FP4X4 = mybir.dt.float4_e2m1fn_x4
+MULT = mybir.AluOpType.mult
+
+P = 128
+PACK = 4
+K, T, N, U = 512, 512, 512, 1024
+FLOPS = 2 * K * N * T
+
+W_CHUNKS = ((0, 64), (64, 96), (96, 128))
+PIECE = 256
+PIECES = U // PIECE
+VECTOR_PIECES = 2
+WORD_STORES = ((0, 512), (512, 768), (768, 1024))
+
+
+def tile_picked_wroute2_linnone_lo_kernel(
+    tc, x_words, x_scales, gate, w1, dst, out_0, out_1, out_2
+):
+    nc = tc.nc
+    with ExitStack() as ctx:
+        keep = ctx.enter_context(tc.tile_pool(name="keep", bufs=1))
+        psum = ctx.enter_context(tc.psum_pool(name="psum", bufs=1))
+
+        w_rows = w1.rearrange("(p j) c -> p j c", j=PACK)
+        w_raw = []
+        for a, (m0, m1) in enumerate(W_CHUNKS):
+            raw = keep.tile([P, PACK, PACK * (m1 - m0)], F32, name=f"w_raw{a}", align_bytes=64)
+            nc.sync.dma_start(out=raw[:], in_=w_rows[:, :, PACK * m0 : PACK * m1])
+            w_raw.append(raw)
+
+        x_codes = keep.tile([P, 2 * T], U8, name="x_codes", align_bytes=64)
+        nc.sync.dma_start(out=x_codes[:].bitcast(I32), in_=x_words[0].bitcast(I32))
+
+        x_plane = keep.tile([P, T], U8, name="x_plane", align_bytes=64)
+        nc.vector.memset(x_plane[:].bitcast(I32), 0)
+        for q in range(4):
+            nc.scalar.dma_start(
+                out=x_plane[32 * q : 32 * q + 4, :].bitcast(I32),
+                in_=x_scales[0, 4 * q : 4 * q + 4, :].bitcast(I32),
+            )
+
+        offsets = keep.tile([P, T // 16], U16, name="offsets")
+        nc.sync.dma_start(offsets[:], dst)
+        gates = keep.tile([P, T], F32, name="gates", align_bytes=64)
+        nc.sync.dma_start(out=gates[:], in_=gate)
+
+        windows = []
+        for t in range(PACK):
+            window = keep.tile([P, U], F32, name=f"window{t}", align_bytes=64)
+            nc.vector.memset(window[:], 0.0)
+            windows.append(window)
+
+        w_first = keep.tile([P, P, PACK], BF16, name="w_first", align_bytes=64)
+        w_rest = keep.tile([P, PACK - 1, P, PACK], BF16, name="w_rest", align_bytes=64)
+        w_codes = keep.tile([P, N], U32, name="w_codes", align_bytes=64)
+        w_plane = keep.tile([P, N], U8, name="w_plane", align_bytes=64)
+        for raw, (m0, m1) in zip(w_raw, W_CHUNKS):
+            dealt = raw[:].rearrange("p j (m t) -> p m t j", t=PACK)
+            nc.vector.tensor_copy(out=w_first[:, m0:m1, :], in_=dealt[:, :, 0, :])
+            nc.vector.tensor_copy(
+                out=w_rest[:, :, m0:m1, :].rearrange("p t m j -> p m t j"), in_=dealt[:, :, 1:, :]
+            )
+        nc.vector.quantize_mx(
+            out=w_codes[:, 0:P].bitcast(FP8X4),
+            scales=w_plane[:, 0:P],
+            in_=w_first[:].rearrange("p m j -> p (m j)"),
+        )
+        w_rest_flat = w_rest[:].rearrange("p t m j -> p (t m j)")
+        for c0, c1 in ((0, P), (P, 3 * P)):
+            nc.vector.quantize_mx(
+                out=w_codes[:, P + c0 : P + c1].bitcast(FP8X4),
+                scales=w_plane[:, P + c0 : P + c1],
+                in_=w_rest_flat[:, PACK * c0 : PACK * c1],
+            )
+
+        results = []
+        for t in range(PACK):
+            bank = psum.tile([P, T], F32, name=f"bank{t}")
+            nc.tensor.matmul_mx(
+                out=bank[:],
+                lhsT=w_codes[:, t * P : (t + 1) * P].bitcast(FP8X4),
+                lhsT_scale=w_plane[:, t * P : (t + 1) * P],
+                rhs=x_codes[:].bitcast(FP4X4),
+                rhs_scale=x_plane[:],
+                start=True,
+                stop=True,
+            )
+            result = keep.tile([P, T], F32, name=f"result{t}", align_bytes=64)
+            nc.scalar.copy(out=result[:], in_=bank[:])
+            results.append(result)
+
+        grouped = [keep.tile([P, PIECE, PACK], BF16, name=f"grouped{a}", align_bytes=64) for a in range(PIECES)]
+        y_codes = keep.tile([P, U], U32, name="y_codes", align_bytes=64)
+        y_plane = keep.tile([P, U], U8, name="y_plane", align_bytes=64)
+        out_rows = out_0.rearrange("(p t) c -> p t c", t=PACK)
+        last = PACK - 1
+        for t in range(PACK):
+            nc.vector.tensor_tensor(windows[t][:].indirect(offsets[:]), results[t][:], gates[:], MULT)
+            nc.sync.dma_start(out=out_rows[:, t, :], in_=windows[t][:])
+            for a in range(PIECES):
+                source = windows[t][:, a * PIECE : (a + 1) * PIECE]
+                if a < VECTOR_PIECES and t == last:
+                    nc.vector.tensor_copy(out=grouped[a][:, :, t], in_=source)
+                elif a < VECTOR_PIECES and t == last - 1:
+                    nc.scalar.copy(out=grouped[a][:, :, t:], in_=source.unsqueeze(2).to_broadcast([P, PIECE, 2]))
+                else:
+                    nc.scalar.copy(out=grouped[a][:, :, t], in_=source)
+
+        for a in range(PIECES):
+            cols = slice(a * PIECE, (a + 1) * PIECE)
+            nc.vector.quantize_mx(
+                out=y_codes[:, cols].bitcast(FP8X4),
+                scales=y_plane[:, cols],
+                in_=grouped[a][:].rearrange("p c t -> p (c t)"),
+            )
+        out_words = out_1[0].rearrange("p c t -> p (c t)").bitcast(I32)
+        for c0, c1 in WORD_STORES:
+            nc.sync.dma_start(out=out_words[:, c0:c1], in_=y_codes[:, c0:c1].bitcast(I32))
+        for q in range(4):
+            queue = nc.scalar if q % 2 == 0 else nc.sync
+            queue.dma_start(
+                out=out_2[0, 4 * q : 4 * q + 4, :].bitcast(I32),
+                in_=y_plane[32 * q : 32 * q + 4, :].bitcast(I32),
+            )

@@ -17,7 +17,8 @@ PACK = 4
 K, T, N, U = 512, 512, 512, 1024
 FLOPS = 2 * K * N * T
 
-W_CHUNKS = ((0, 64), (64, 96), (96, 128))
+T_GROUPS = ((0, 1), (1, 2), (2, 4))
+FIRST = 128
 PIECE = 256
 PIECES = U // PIECE
 VECTOR_PIECES = 2
@@ -32,11 +33,11 @@ def tile_picked_wroute2_linnone_lo_kernel(
         keep = ctx.enter_context(tc.tile_pool(name="keep", bufs=1))
         psum = ctx.enter_context(tc.psum_pool(name="psum", bufs=1))
 
-        w_rows = w1.rearrange("(p j) c -> p j c", j=PACK)
+        w_pairs = w1.rearrange("(p u e) c -> p u e c", u=2, e=2)
         w_raw = []
-        for a, (m0, m1) in enumerate(W_CHUNKS):
-            raw = keep.tile([P, PACK, PACK * (m1 - m0)], F32, name=f"w_raw{a}", align_bytes=64)
-            nc.sync.dma_start(out=raw[:], in_=w_rows[:, :, PACK * m0 : PACK * m1])
+        for u in range(2):
+            raw = keep.tile([P, 2, N], F32, name=f"w_raw{u}", align_bytes=64)
+            nc.sync.dma_start(out=raw[:], in_=w_pairs[:, u, :, :])
             w_raw.append(raw)
 
         x_codes = keep.tile([P, 2 * T], U8, name="x_codes", align_bytes=64)
@@ -58,47 +59,59 @@ def tile_picked_wroute2_linnone_lo_kernel(
         windows = []
         for t in range(PACK):
             window = keep.tile([P, U], F32, name=f"window{t}", align_bytes=64)
-            nc.vector.memset(window[:], 0.0)
+            (nc.vector if t < 2 else nc.gpsimd).memset(window[:], 0.0)
             windows.append(window)
 
-        w_first = keep.tile([P, P, PACK], BF16, name="w_first", align_bytes=64)
-        w_rest = keep.tile([P, PACK - 1, P, PACK], BF16, name="w_rest", align_bytes=64)
+        w_grouped = [
+            keep.tile([P, t1 - t0, P, PACK], BF16, name=f"w_grouped{t0}", align_bytes=64) for t0, t1 in T_GROUPS
+        ]
         w_codes = keep.tile([P, N], U32, name="w_codes", align_bytes=64)
         w_plane = keep.tile([P, N], U8, name="w_plane", align_bytes=64)
-        for raw, (m0, m1) in zip(w_raw, W_CHUNKS):
-            dealt = raw[:].rearrange("p j (m t) -> p m t j", t=PACK)
-            nc.vector.tensor_copy(out=w_first[:, m0:m1, :], in_=dealt[:, :, 0, :])
-            nc.vector.tensor_copy(
-                out=w_rest[:, :, m0:m1, :].rearrange("p t m j -> p m t j"), in_=dealt[:, :, 1:, :]
-            )
-        nc.vector.quantize_mx(
-            out=w_codes[:, 0:P].bitcast(FP8X4),
-            scales=w_plane[:, 0:P],
-            in_=w_first[:].rearrange("p m j -> p (m j)"),
-        )
-        w_rest_flat = w_rest[:].rearrange("p t m j -> p (t m j)")
-        for c0, c1 in ((0, P), (P, 3 * P)):
-            nc.vector.quantize_mx(
-                out=w_codes[:, P + c0 : P + c1].bitcast(FP8X4),
-                scales=w_plane[:, P + c0 : P + c1],
-                in_=w_rest_flat[:, PACK * c0 : PACK * c1],
+
+        def deal(copy, u, g):
+            t0, t1 = T_GROUPS[g]
+            copy(
+                out=w_grouped[g][:, :, :, 2 * u : 2 * u + 2].rearrange("p t m e -> p m t e"),
+                in_=w_raw[u][:].rearrange("p e (m t) -> p m t e", t=PACK)[:, :, t0:t1, :],
             )
 
-        results = []
-        for t in range(PACK):
-            bank = psum.tile([P, T], F32, name=f"bank{t}")
-            nc.tensor.matmul_mx(
-                out=bank[:],
-                lhsT=w_codes[:, t * P : (t + 1) * P].bitcast(FP8X4),
-                lhsT_scale=w_plane[:, t * P : (t + 1) * P],
-                rhs=x_codes[:].bitcast(FP4X4),
-                rhs_scale=x_plane[:],
-                start=True,
-                stop=True,
+        def quantize_w(g):
+            t0, t1 = T_GROUPS[g]
+            nc.vector.quantize_mx(
+                out=w_codes[:, t0 * P : t1 * P].bitcast(FP8X4),
+                scales=w_plane[:, t0 * P : t1 * P],
+                in_=w_grouped[g][:].rearrange("p t m j -> p (t m j)"),
             )
-            result = keep.tile([P, T], F32, name=f"result{t}", align_bytes=64)
-            nc.scalar.copy(out=result[:], in_=bank[:])
-            results.append(result)
+
+        for g in range(3):
+            deal(nc.vector.tensor_copy, 0, g)
+        deal(nc.vector.tensor_copy, 1, 0)
+        deal(nc.vector.tensor_copy, 1, 1)
+        deal(nc.scalar.copy, 1, 2)
+        quantize_w(0)
+        quantize_w(1)
+        quantize_w(2)
+
+        def product(t, name, cuts):
+            c0, c1 = cuts[0], cuts[-1]
+            bank = psum.tile([P, T], F32, name=f"bank{name}")
+            for a, b in zip(cuts, cuts[1:]):
+                nc.tensor.matmul_mx(
+                    out=bank[:, a - c0 : b - c0],
+                    lhsT=w_codes[:, t * P : (t + 1) * P].bitcast(FP8X4),
+                    lhsT_scale=w_plane[:, t * P : (t + 1) * P],
+                    rhs=x_codes[:, 2 * a : 2 * b].bitcast(FP4X4),
+                    rhs_scale=x_plane[:, a:b],
+                    start=True,
+                    stop=True,
+                )
+            result = keep.tile([P, c1 - c0], F32, name=f"result{name}", align_bytes=64)
+            nc.scalar.copy(out=result[:], in_=bank[:, 0 : c1 - c0])
+            return (result, c0, c1)
+
+        results = [[product(0, "0a", (0, FIRST)), product(0, "0b", (FIRST, 2 * FIRST, T))]]
+        for t in range(1, PACK):
+            results.append([product(t, str(t), (0, T))])
 
         grouped = [keep.tile([P, PIECE, PACK], BF16, name=f"grouped{a}", align_bytes=64) for a in range(PIECES)]
         y_codes = keep.tile([P, U], U32, name="y_codes", align_bytes=64)
@@ -106,7 +119,10 @@ def tile_picked_wroute2_linnone_lo_kernel(
         out_rows = out_0.rearrange("(p t) c -> p t c", t=PACK)
         last = PACK - 1
         for t in range(PACK):
-            nc.vector.tensor_tensor(windows[t][:].indirect(offsets[:]), results[t][:], gates[:], MULT)
+            for result, c0, c1 in results[t]:
+                nc.vector.tensor_tensor(
+                    windows[t][:].indirect(offsets[:, c0 // 16 : c1 // 16]), result[:], gates[:, c0:c1], MULT
+                )
             nc.sync.dma_start(out=out_rows[:, t, :], in_=windows[t][:])
             for a in range(PIECES):
                 source = windows[t][:, a * PIECE : (a + 1) * PIECE]

@@ -20,8 +20,7 @@ FLOPS = 2 * K * N * T
 T_GROUPS = ((0, 1), (1, 2), (2, 4))
 FIRST = 128
 PIECE = 256
-PIECES = U // PIECE
-VECTOR_PIECES = 2
+SPLIT = 512
 WORD_STORES = ((0, 512), (512, 768), (768, 1024))
 
 
@@ -113,7 +112,7 @@ def tile_picked_wroute2_linnone_lo_kernel(
         for t in range(1, PACK):
             results.append([product(t, str(t), (0, T))])
 
-        grouped = [keep.tile([P, PIECE, PACK], BF16, name=f"grouped{a}", align_bytes=64) for a in range(PIECES)]
+        grouped = keep.tile([P, U, PACK], BF16, name="grouped", align_bytes=64)
         y_codes = keep.tile([P, U], U32, name="y_codes", align_bytes=64)
         y_plane = keep.tile([P, U], U8, name="y_plane", align_bytes=64)
         out_rows = out_0.rearrange("(p t) c -> p t c", t=PACK)
@@ -124,21 +123,24 @@ def tile_picked_wroute2_linnone_lo_kernel(
                     windows[t][:].indirect(offsets[:, c0 // 16 : c1 // 16]), result[:], gates[:, c0:c1], MULT
                 )
             nc.sync.dma_start(out=out_rows[:, t, :], in_=windows[t][:])
-            for a in range(PIECES):
-                source = windows[t][:, a * PIECE : (a + 1) * PIECE]
-                if a < VECTOR_PIECES and t == last:
-                    nc.vector.tensor_copy(out=grouped[a][:, :, t], in_=source)
-                elif a < VECTOR_PIECES and t == last - 1:
-                    nc.scalar.copy(out=grouped[a][:, :, t:], in_=source.unsqueeze(2).to_broadcast([P, PIECE, 2]))
-                else:
-                    nc.scalar.copy(out=grouped[a][:, :, t], in_=source)
+            if t < last - 1:
+                nc.scalar.copy(out=grouped[:, :, t], in_=windows[t][:])
+            elif t < last:
+                nc.scalar.copy(
+                    out=grouped[:, :SPLIT, t:], in_=windows[t][:, :SPLIT].unsqueeze(2).to_broadcast([P, SPLIT, 2])
+                )
+                nc.scalar.copy(out=grouped[:, SPLIT:, t], in_=windows[t][:, SPLIT:])
+            else:
+                for c0 in range(0, U, PIECE):
+                    copy = nc.vector.tensor_copy if c0 < SPLIT else nc.scalar.copy
+                    copy(out=grouped[:, c0 : c0 + PIECE, t], in_=windows[t][:, c0 : c0 + PIECE])
 
-        for a in range(PIECES):
-            cols = slice(a * PIECE, (a + 1) * PIECE)
+        grouped_flat = grouped[:].rearrange("p c t -> p (c t)")
+        for c0 in range(0, U, PIECE):
             nc.vector.quantize_mx(
-                out=y_codes[:, cols].bitcast(FP8X4),
-                scales=y_plane[:, cols],
-                in_=grouped[a][:].rearrange("p c t -> p (c t)"),
+                out=y_codes[:, c0 : c0 + PIECE].bitcast(FP8X4),
+                scales=y_plane[:, c0 : c0 + PIECE],
+                in_=grouped_flat[:, PACK * c0 : PACK * (c0 + PIECE)],
             )
         out_words = out_1[0].rearrange("p c t -> p (c t)").bitcast(I32)
         for c0, c1 in WORD_STORES:

@@ -19,9 +19,9 @@ FLOPS = 2 * K * N * T
 
 T_GROUPS = ((0, 1), (1, 2), (2, 4))
 FIRST = 128
-PIECE = 256
+PIECES = ((0, 256), (256, 512), (512, 640), (640, 896), (896, 1024))
 SPLIT = 512
-WORD_STORES = ((0, 512), (512, 768), (768, 1024))
+WORD_STORES = ((0, 256), (256, 640), (640, 1024))
 
 
 def tile_picked_wroute2_linnone_lo_kernel(
@@ -33,32 +33,28 @@ def tile_picked_wroute2_linnone_lo_kernel(
         psum = ctx.enter_context(tc.psum_pool(name="psum", bufs=1))
 
         w_pairs = w1.rearrange("(p u e) c -> p u e c", u=2, e=2)
-        w_raw = []
-        for u in range(2):
-            raw = keep.tile([P, 2, N], F32, name=f"w_raw{u}", align_bytes=64)
-            nc.sync.dma_start(out=raw[:], in_=w_pairs[:, u, :, :])
-            w_raw.append(raw)
-
-        x_codes = keep.tile([P, 2 * T], U8, name="x_codes", align_bytes=64)
-        nc.sync.dma_start(out=x_codes[:].bitcast(I32), in_=x_words[0].bitcast(I32))
-
+        w_raw = [keep.tile([P, 2, N], F32, name=f"w_raw{u}", align_bytes=64) for u in range(2)]
+        offsets = keep.tile([P, T // 16], U16, name="offsets")
         x_plane = keep.tile([P, T], U8, name="x_plane", align_bytes=64)
+        x_codes = keep.tile([P, 2 * T], U8, name="x_codes", align_bytes=64)
+        gates = keep.tile([P, T], F32, name="gates", align_bytes=64)
+
         nc.vector.memset(x_plane[:].bitcast(I32), 0)
+        nc.sync.dma_start(out=w_raw[0][:], in_=w_pairs[:, 0, :, :])
+        nc.sync.dma_start(offsets[:], dst)
         for q in range(4):
-            nc.scalar.dma_start(
+            nc.sync.dma_start(
                 out=x_plane[32 * q : 32 * q + 4, :].bitcast(I32),
                 in_=x_scales[0, 4 * q : 4 * q + 4, :].bitcast(I32),
             )
-
-        offsets = keep.tile([P, T // 16], U16, name="offsets")
-        nc.sync.dma_start(offsets[:], dst)
-        gates = keep.tile([P, T], F32, name="gates", align_bytes=64)
+        nc.sync.dma_start(out=w_raw[1][:], in_=w_pairs[:, 1, :, :])
+        nc.sync.dma_start(out=x_codes[:].bitcast(I32), in_=x_words[0].bitcast(I32))
         nc.sync.dma_start(out=gates[:], in_=gate)
 
         windows = []
         for t in range(PACK):
             window = keep.tile([P, U], F32, name=f"window{t}", align_bytes=64)
-            (nc.vector if t < 2 else nc.gpsimd).memset(window[:], 0.0)
+            nc.vector.memset(window[:], 0.0)
             windows.append(window)
 
         w_grouped = [
@@ -131,22 +127,22 @@ def tile_picked_wroute2_linnone_lo_kernel(
                 )
                 nc.scalar.copy(out=grouped[:, SPLIT:, t], in_=windows[t][:, SPLIT:])
             else:
-                for c0 in range(0, U, PIECE):
+                for c0, c1 in PIECES:
                     copy = nc.vector.tensor_copy if c0 < SPLIT else nc.scalar.copy
-                    copy(out=grouped[:, c0 : c0 + PIECE, t], in_=windows[t][:, c0 : c0 + PIECE])
+                    copy(out=grouped[:, c0:c1, t], in_=windows[t][:, c0:c1])
 
         grouped_flat = grouped[:].rearrange("p c t -> p (c t)")
-        for c0 in range(0, U, PIECE):
+        for c0, c1 in PIECES:
             nc.vector.quantize_mx(
-                out=y_codes[:, c0 : c0 + PIECE].bitcast(FP8X4),
-                scales=y_plane[:, c0 : c0 + PIECE],
-                in_=grouped_flat[:, PACK * c0 : PACK * (c0 + PIECE)],
+                out=y_codes[:, c0:c1].bitcast(FP8X4),
+                scales=y_plane[:, c0:c1],
+                in_=grouped_flat[:, PACK * c0 : PACK * c1],
             )
         out_words = out_1[0].rearrange("p c t -> p (c t)").bitcast(I32)
         for c0, c1 in WORD_STORES:
             nc.sync.dma_start(out=out_words[:, c0:c1], in_=y_codes[:, c0:c1].bitcast(I32))
         for q in range(4):
-            queue = nc.scalar if q % 2 == 0 else nc.sync
+            queue = nc.scalar if q < 3 else nc.sync
             queue.dma_start(
                 out=out_2[0, 4 * q : 4 * q + 4, :].bitcast(I32),
                 in_=y_plane[32 * q : 32 * q + 4, :].bitcast(I32),

@@ -41,20 +41,20 @@ def tile_picked_wroute2_linnone_lo_kernel(
 
         nc.vector.memset(x_plane[:].bitcast(I32), 0)
         nc.sync.dma_start(out=w_raw[0][:], in_=w_pairs[:, 0, :, :])
+        nc.sync.dma_start(out=w_raw[1][:], in_=w_pairs[:, 1, :, :])
         nc.sync.dma_start(offsets[:], dst)
         for q in range(4):
             nc.sync.dma_start(
                 out=x_plane[32 * q : 32 * q + 4, :].bitcast(I32),
                 in_=x_scales[0, 4 * q : 4 * q + 4, :].bitcast(I32),
             )
-        nc.sync.dma_start(out=w_raw[1][:], in_=w_pairs[:, 1, :, :])
         nc.sync.dma_start(out=x_codes[:].bitcast(I32), in_=x_words[0].bitcast(I32))
         nc.sync.dma_start(out=gates[:], in_=gate)
 
         windows = []
         for t in range(PACK):
             window = keep.tile([P, U], F32, name=f"window{t}", align_bytes=64)
-            nc.vector.memset(window[:], 0.0)
+            nc.vector.memset(window[:].bitcast(I32), 0)
             windows.append(window)
 
         w_grouped = [

@@ -18,10 +18,14 @@ K, T, N, U = 512, 512, 512, 1024
 FLOPS = 2 * K * N * T
 
 T_GROUPS = ((0, 1), (1, 2), (2, 4))
+SLOTS = (0, 2, 1, 3)
+SLOT_SLICES = (slice(0, 1), slice(2, 3), slice(1, 4, 2))
 FIRST = 128
-PIECES = ((0, 256), (256, 512), (512, 640), (640, 896), (896, 1024))
+COPIES = ((0, 256), (256, 512), (512, 768), (768, 896), (896, 1024))
+PIECES = ((0, 256), (256, 384), (384, 512), (512, 768), (768, 896), (896, 1024))
 SPLIT = 512
-WORD_STORES = ((0, 256), (256, 640), (640, 1024))
+FILL = 128
+WORD_STORES = ((0, 384), (384, 768), (768, 1024))
 
 
 def tile_picked_wroute2_linnone_lo_kernel(
@@ -52,7 +56,7 @@ def tile_picked_wroute2_linnone_lo_kernel(
         nc.sync.dma_start(out=gates[:], in_=gate)
 
         windows = []
-        for t in range(PACK):
+        for t in range(2):
             window = keep.tile([P, U], F32, name=f"window{t}", align_bytes=64)
             nc.vector.memset(window[:].bitcast(I32), 0)
             windows.append(window)
@@ -64,10 +68,9 @@ def tile_picked_wroute2_linnone_lo_kernel(
         w_plane = keep.tile([P, N], U8, name="w_plane", align_bytes=64)
 
         def deal(copy, u, g):
-            t0, t1 = T_GROUPS[g]
             copy(
                 out=w_grouped[g][:, :, :, 2 * u : 2 * u + 2].rearrange("p t m e -> p m t e"),
-                in_=w_raw[u][:].rearrange("p e (m t) -> p m t e", t=PACK)[:, :, t0:t1, :],
+                in_=w_raw[u][:].rearrange("p e (m t) -> p m t e", t=PACK)[:, :, SLOT_SLICES[g], :],
             )
 
         def quantize_w(g):
@@ -108,7 +111,12 @@ def tile_picked_wroute2_linnone_lo_kernel(
         for t in range(1, PACK):
             results.append([product(t, str(t), (0, T))])
 
-        grouped = keep.tile([P, U, PACK], BF16, name="grouped", align_bytes=64)
+        for t, tag in ((2, "w_codes"), (3, "x_plane")):
+            window = keep.tile([P, U], F32, name=f"window{t}", tag=tag, align_bytes=64)
+            nc.gpsimd.memset(window[:].bitcast(I32), 0)
+            windows.append(window)
+
+        grouped = keep.tile([P, U, PACK], BF16, name="grouped", tag="x_codes", align_bytes=64)
         y_codes = keep.tile([P, U], U32, name="y_codes", align_bytes=64)
         y_plane = keep.tile([P, U], U8, name="y_plane", align_bytes=64)
         out_rows = out_0.rearrange("(p t) c -> p t c", t=PACK)
@@ -118,18 +126,22 @@ def tile_picked_wroute2_linnone_lo_kernel(
                 nc.vector.tensor_tensor(
                     windows[t][:].indirect(offsets[:, c0 // 16 : c1 // 16]), result[:], gates[:, c0:c1], MULT
                 )
-            nc.sync.dma_start(out=out_rows[:, t, :], in_=windows[t][:])
-            if t < last - 1:
-                nc.scalar.copy(out=grouped[:, :, t], in_=windows[t][:])
-            elif t < last:
+            slot = SLOTS[t]
+            nc.sync.dma_start(out=out_rows[:, slot, :], in_=windows[t][:])
+            if t < 2:
+                shared = FILL if t == 0 else SPLIT
+                nc.scalar.copy(out=grouped[:, shared:, slot], in_=windows[t][:, shared:])
                 nc.scalar.copy(
-                    out=grouped[:, :SPLIT, t:], in_=windows[t][:, :SPLIT].unsqueeze(2).to_broadcast([P, SPLIT, 2])
+                    out=grouped[:, :shared, slot : slot + 2],
+                    in_=windows[t][:, :shared].unsqueeze(2).to_broadcast([P, shared, 2]),
                 )
-                nc.scalar.copy(out=grouped[:, SPLIT:, t], in_=windows[t][:, SPLIT:])
+            elif t < last:
+                nc.scalar.copy(out=grouped[:, FILL:, slot], in_=windows[t][:, FILL:])
             else:
-                for c0, c1 in PIECES:
+                nc.vector.tensor_copy(out=grouped[:, :FILL, SLOTS[t - 1]], in_=windows[t - 1][:, :FILL])
+                for c0, c1 in COPIES:
                     copy = nc.vector.tensor_copy if c0 < SPLIT else nc.scalar.copy
-                    copy(out=grouped[:, c0:c1, t], in_=windows[t][:, c0:c1])
+                    copy(out=grouped[:, c0:c1, slot], in_=windows[t][:, c0:c1])
 
         grouped_flat = grouped[:].rearrange("p c t -> p (c t)")
         for c0, c1 in PIECES:

@@ -21,9 +21,9 @@ T_GROUPS = ((0, 1), (1, 2), (2, 4))
 SLOTS = (0, 2, 1, 3)
 SLOT_SLICES = (slice(0, 1), slice(2, 3), slice(1, 4, 2))
 FIRST = 128
-COPIES = ((0, 256), (256, 512), (512, 768), (768, 896), (896, 1024))
+COPIES = ((0, 256), (256, 576), (576, 768), (768, 896), (896, 1024))
 PIECES = ((0, 256), (256, 384), (384, 512), (512, 768), (768, 896), (896, 1024))
-SPLIT = 512
+SPLIT = 576
 FILL = 128
 WORD_STORES = ((0, 384), (384, 768), (768, 1024))
 
@@ -107,9 +107,9 @@ def tile_picked_wroute2_linnone_lo_kernel(
             nc.scalar.copy(out=result[:], in_=bank[:, 0 : c1 - c0])
             return (result, c0, c1)
 
-        results = [[product(0, "0a", (0, FIRST)), product(0, "0b", (FIRST, 2 * FIRST, T))]]
-        for t in range(1, PACK):
-            results.append([product(t, str(t), (0, T))])
+        heads = [product(t, f"{t}a", (0, FIRST)) for t in range(2)]
+        results = [product(t, f"{t}b", (FIRST, 2 * FIRST, T)) for t in range(2)]
+        results = results + [product(t, str(t), (0, T)) for t in range(2, PACK)]
 
         for t, tag in ((2, "w_codes"), (3, "x_plane")):
             window = keep.tile([P, U], F32, name=f"window{t}", tag=tag, align_bytes=64)
@@ -121,11 +121,17 @@ def tile_picked_wroute2_linnone_lo_kernel(
         y_plane = keep.tile([P, U], U8, name="y_plane", align_bytes=64)
         out_rows = out_0.rearrange("(p t) c -> p t c", t=PACK)
         last = PACK - 1
+
+        def scatter(t, piece):
+            result, c0, c1 = piece
+            nc.vector.tensor_tensor(
+                windows[t][:].indirect(offsets[:, c0 // 16 : c1 // 16]), result[:], gates[:, c0:c1], MULT
+            )
+
+        for t in range(2):
+            scatter(t, heads[t])
         for t in range(PACK):
-            for result, c0, c1 in results[t]:
-                nc.vector.tensor_tensor(
-                    windows[t][:].indirect(offsets[:, c0 // 16 : c1 // 16]), result[:], gates[:, c0:c1], MULT
-                )
+            scatter(t, results[t])
             slot = SLOTS[t]
             nc.sync.dma_start(out=out_rows[:, slot, :], in_=windows[t][:])
             if t < 2:

@@ -18,13 +18,14 @@ K, T, N, U = 512, 512, 512, 1024
 FLOPS = 2 * K * N * T
 
 T_GROUPS = ((0, 1), (1, 2), (2, 4))
-SLOTS = (0, 2, 1, 3)
-SLOT_SLICES = (slice(0, 1), slice(2, 3), slice(1, 4, 2))
+SLOT_SLICES = (slice(0, 1), slice(1, 2), slice(2, 4))
 FIRST = 128
-COPIES = ((0, 256), (256, 576), (576, 768), (768, 896), (896, 1024))
+COPIES = ((0, 256), (256, 512), (512, 768), (768, 896), (896, 1024))
 PIECES = ((0, 256), (256, 384), (384, 512), (512, 768), (768, 896), (896, 1024))
-SPLIT = 576
+SPLIT = 512
 FILL = 128
+STAGED = 512
+WHOLE = (240, 272)
 WORD_STORES = ((0, 384), (384, 768), (768, 1024))
 
 
@@ -111,12 +112,13 @@ def tile_picked_wroute2_linnone_lo_kernel(
         results = [product(t, f"{t}b", (FIRST, 2 * FIRST, T)) for t in range(2)]
         results = results + [product(t, str(t), (0, T)) for t in range(2, PACK)]
 
-        for t, tag in ((2, "w_codes"), (3, "x_plane")):
+        for t, tag in ((2, "w_codes"), (3, "w_plane")):
             window = keep.tile([P, U], F32, name=f"window{t}", tag=tag, align_bytes=64)
             nc.gpsimd.memset(window[:].bitcast(I32), 0)
             windows.append(window)
 
-        grouped = keep.tile([P, U, PACK], BF16, name="grouped", tag="x_codes", align_bytes=64)
+        pairs = keep.tile([P, STAGED, 2], BF16, name="pairs", tag="x_codes", align_bytes=64)
+        grouped = keep.tile([P, U, PACK], BF16, name="grouped", tag="x_plane", align_bytes=64)
         y_codes = keep.tile([P, U], U32, name="y_codes", align_bytes=64)
         y_plane = keep.tile([P, U], U8, name="y_plane", align_bytes=64)
         out_rows = out_0.rearrange("(p t) c -> p t c", t=PACK)
@@ -132,19 +134,30 @@ def tile_picked_wroute2_linnone_lo_kernel(
             scatter(t, heads[t])
         for t in range(PACK):
             scatter(t, results[t])
-            slot = SLOTS[t]
+            slot = t
             nc.sync.dma_start(out=out_rows[:, slot, :], in_=windows[t][:])
             if t < 2:
-                shared = FILL if t == 0 else SPLIT
-                nc.scalar.copy(out=grouped[:, shared:, slot], in_=windows[t][:, shared:])
+                nc.scalar.copy(out=pairs[:, :, slot], in_=windows[t][:, :STAGED])
+            if t == 0:
+                nc.scalar.copy(out=grouped[:, STAGED:, slot], in_=windows[t][:, STAGED:])
+            if t == 1:
+                nc.scalar.copy(out=grouped[:, STAGED:768, slot], in_=windows[t][:, STAGED:768])
                 nc.scalar.copy(
-                    out=grouped[:, :shared, slot : slot + 2],
-                    in_=windows[t][:, :shared].unsqueeze(2).to_broadcast([P, shared, 2]),
+                    out=grouped[:, :STAGED, :].bitcast(U32),
+                    in_=pairs[:].bitcast(U32).to_broadcast([P, STAGED, 2]),
                 )
-            elif t < last:
-                nc.scalar.copy(out=grouped[:, FILL:, slot], in_=windows[t][:, FILL:])
-            else:
-                nc.vector.tensor_copy(out=grouped[:, :FILL, SLOTS[t - 1]], in_=windows[t - 1][:, :FILL])
+                nc.scalar.copy(out=grouped[:, 768:, slot], in_=windows[t][:, 768:])
+            if t == 2:
+                w0, w1_ = WHOLE
+                nc.scalar.copy(out=grouped[:, FILL:w0, slot], in_=windows[t][:, FILL:w0])
+                nc.scalar.copy(out=grouped[:, w1_:SPLIT, slot], in_=windows[t][:, w1_:SPLIT])
+                nc.scalar.copy(
+                    out=grouped[:, w0:w1_, slot : slot + 2],
+                    in_=windows[t][:, w0:w1_].unsqueeze(2).to_broadcast([P, w1_ - w0, 2]),
+                )
+                nc.scalar.copy(out=grouped[:, SPLIT:, slot], in_=windows[t][:, SPLIT:])
+            if t == last:
+                nc.vector.tensor_copy(out=grouped[:, :FILL, t - 1], in_=windows[t - 1][:, :FILL])
                 for c0, c1 in COPIES:
                     copy = nc.vector.tensor_copy if c0 < SPLIT else nc.scalar.copy
                     copy(out=grouped[:, c0:c1, slot], in_=windows[t][:, c0:c1])

@@ -20,9 +20,9 @@ FLOPS = 2 * K * N * T
 T_GROUPS = ((0, 1), (1, 2), (2, 4))
 SLOT_SLICES = (slice(0, 1), slice(1, 2), slice(2, 4))
 FIRST = 128
-COPIES = ((0, 256), (256, 512), (512, 768), (768, 896), (896, 1024))
-PIECES = ((0, 256), (256, 384), (384, 512), (512, 768), (768, 896), (896, 1024))
-SPLIT = 512
+COPIES = ((0, 256), (256, 480), (480, 768), (768, 896), (896, 960), (960, 1024))
+PIECES = ((0, 256), (256, 384), (384, 512), (512, 768), (768, 896), (896, 960), (960, 1024))
+SPLIT = 480
 FILL = 128
 STAGED = 512
 WHOLE = (240, 272)

@@ -11,6 +11,7 @@ U8 = mybir.dt.uint8
 FP8X4 = mybir.dt.float8_e4m3fn_x4
 FP4X4 = mybir.dt.float4_e2m1fn_x4
 MULT = mybir.AluOpType.mult
+COPY = mybir.ActivationFunctionType.Copy
 
 P = 128
 PACK = 4
@@ -18,15 +19,10 @@ K, T, N, U = 512, 512, 512, 1024
 FLOPS = 2 * K * N * T
 
 T_GROUPS = ((0, 1), (1, 2), (2, 4))
-SLOT_SLICES = (slice(0, 1), slice(1, 2), slice(2, 4))
 FIRST = 128
-COPIES = ((0, 256), (256, 480), (480, 768), (768, 896), (896, 960), (960, 1024))
-PIECES = ((0, 256), (256, 384), (384, 512), (512, 768), (768, 896), (896, 960), (960, 1024))
-SPLIT = 480
-FILL = 128
-STAGED = 512
-WHOLE = (240, 272)
-WORD_STORES = ((0, 384), (384, 768), (768, 1024))
+BLOCK = 128
+RANGES = ((0, 128), (128, 384), (384, 640), (640, 896), (896, 1024))
+WORD_STORES = ((0, 384), (384, 640), (640, 1024))
 
 
 def tile_picked_wroute2_linnone_lo_kernel(
@@ -69,9 +65,10 @@ def tile_picked_wroute2_linnone_lo_kernel(
         w_plane = keep.tile([P, N], U8, name="w_plane", align_bytes=64)
 
         def deal(copy, u, g):
+            t0, t1 = T_GROUPS[g]
             copy(
                 out=w_grouped[g][:, :, :, 2 * u : 2 * u + 2].rearrange("p t m e -> p m t e"),
-                in_=w_raw[u][:].rearrange("p e (m t) -> p m t e", t=PACK)[:, :, SLOT_SLICES[g], :],
+                in_=w_raw[u][:].rearrange("p e (m t) -> p m t e", t=PACK)[:, :, t0:t1, :],
             )
 
         def quantize_w(g):
@@ -104,71 +101,84 @@ def tile_picked_wroute2_linnone_lo_kernel(
                     start=True,
                     stop=True,
                 )
-            result = keep.tile([P, c1 - c0], F32, name=f"result{name}", align_bytes=64)
-            nc.scalar.copy(out=result[:], in_=bank[:, 0 : c1 - c0])
-            return (result, c0, c1)
+            gated = keep.tile([P, c1 - c0], F32, name=f"gated{name}", align_bytes=64)
+            nc.vector.tensor_tensor(gated[:], bank[:, 0 : c1 - c0], gates[:, c0:c1], MULT)
+            return gated
 
-        heads = [product(t, f"{t}a", (0, FIRST)) for t in range(2)]
-        results = [product(t, f"{t}b", (FIRST, 2 * FIRST, T)) for t in range(2)]
-        results = results + [product(t, str(t), (0, T)) for t in range(2, PACK)]
+        head0 = product(0, "0a", (0, FIRST))
+        head1 = product(1, "1a", (0, FIRST))
+        rest0 = product(0, "0b", (FIRST, 2 * FIRST, T))
+        rest1 = product(1, "1b", (FIRST, 2 * FIRST, T))
+        whole2 = product(2, "2", (0, T))
+        whole3 = product(3, "3", (0, T))
 
-        for t, tag in ((2, "w_codes"), (3, "w_plane")):
+        out_rows = out_0.rearrange("(p t) c -> p t c", t=PACK)
+
+        def on_scalar(t, values, c0, c1):
+            nc.scalar.activation(windows[t][:].indirect(offsets[:, c0 // 16 : c1 // 16]), values, COPY)
+
+        def on_vector(t, values, c0, c1):
+            nc.vector.tensor_copy(windows[t][:].indirect(offsets[:, c0 // 16 : c1 // 16]), values)
+
+        def store(t):
+            nc.sync.dma_start(out=out_rows[:, t, :], in_=windows[t][:])
+
+        on_scalar(0, head0[:], 0, FIRST)
+        for t, tag in ((2, "w_grouped2"), (3, "gated0a")):
             window = keep.tile([P, U], F32, name=f"window{t}", tag=tag, align_bytes=64)
             nc.gpsimd.memset(window[:].bitcast(I32), 0)
             windows.append(window)
+        on_scalar(1, head1[:], 0, FIRST)
+        on_scalar(0, rest0[:], FIRST, T)
+        store(0)
+        on_vector(2, whole2[:, :FIRST], 0, FIRST)
+        on_vector(3, whole3[:], 0, T)
+        on_scalar(1, rest1[:], FIRST, T)
+        store(1)
+        store(3)
+        on_scalar(2, whole2[:, FIRST:], FIRST, T)
+        store(2)
 
-        pairs = keep.tile([P, STAGED, 2], BF16, name="pairs", tag="x_codes", align_bytes=64)
-        grouped = keep.tile([P, U, PACK], BF16, name="grouped", tag="x_plane", align_bytes=64)
-        y_codes = keep.tile([P, U], U32, name="y_codes", align_bytes=64)
-        y_plane = keep.tile([P, U], U8, name="y_plane", align_bytes=64)
-        out_rows = out_0.rearrange("(p t) c -> p t c", t=PACK)
-        last = PACK - 1
+        pairs = keep.tile([P, U // BLOCK, 2, BLOCK, 2], BF16, name="pairs", tag="gated3", align_bytes=64)
 
-        def scatter(t, piece):
-            result, c0, c1 = piece
-            nc.vector.tensor_tensor(
-                windows[t][:].indirect(offsets[:, c0 // 16 : c1 // 16]), result[:], gates[:, c0:c1], MULT
+        def stage(t, c0, c1):
+            nc.vector.tensor_copy(
+                out=pairs[:, c0 // BLOCK : c1 // BLOCK, t // 2, :, t % 2],
+                in_=windows[t][:, c0:c1].rearrange("p (b c) -> p b c", c=BLOCK),
             )
 
-        for t in range(2):
-            scatter(t, heads[t])
-        for t in range(PACK):
-            scatter(t, results[t])
-            slot = t
-            nc.sync.dma_start(out=out_rows[:, slot, :], in_=windows[t][:])
-            if t < 2:
-                nc.scalar.copy(out=pairs[:, :, slot], in_=windows[t][:, :STAGED])
-            if t == 0:
-                nc.scalar.copy(out=grouped[:, STAGED:, slot], in_=windows[t][:, STAGED:])
-            if t == 1:
-                nc.scalar.copy(out=grouped[:, STAGED:768, slot], in_=windows[t][:, STAGED:768])
-                nc.scalar.copy(
-                    out=grouped[:, :STAGED, :].bitcast(U32),
-                    in_=pairs[:].bitcast(U32).to_broadcast([P, STAGED, 2]),
-                )
-                nc.scalar.copy(out=grouped[:, 768:, slot], in_=windows[t][:, 768:])
-            if t == 2:
-                w0, w1_ = WHOLE
-                nc.scalar.copy(out=grouped[:, FILL:w0, slot], in_=windows[t][:, FILL:w0])
-                nc.scalar.copy(out=grouped[:, w1_:SPLIT, slot], in_=windows[t][:, w1_:SPLIT])
-                nc.scalar.copy(
-                    out=grouped[:, w0:w1_, slot : slot + 2],
-                    in_=windows[t][:, w0:w1_].unsqueeze(2).to_broadcast([P, w1_ - w0, 2]),
-                )
-                nc.scalar.copy(out=grouped[:, SPLIT:, slot], in_=windows[t][:, SPLIT:])
-            if t == last:
-                nc.vector.tensor_copy(out=grouped[:, :FILL, t - 1], in_=windows[t - 1][:, :FILL])
-                for c0, c1 in COPIES:
-                    copy = nc.vector.tensor_copy if c0 < SPLIT else nc.scalar.copy
-                    copy(out=grouped[:, c0:c1, slot], in_=windows[t][:, c0:c1])
+        for t in (0, 3, 1):
+            stage(t, 0, U)
+        for c0, c1 in RANGES:
+            stage(2, c0, c1)
 
-        grouped_flat = grouped[:].rearrange("p c t -> p (c t)")
-        for c0, c1 in PIECES:
+        y_codes = keep.tile([P, U], U32, name="y_codes", align_bytes=64)
+        y_plane = keep.tile([P, U], U8, name="y_plane", align_bytes=64)
+        grouped = [keep.tile([P, c1 - c0, PACK], BF16, name=f"grouped{c0}", align_bytes=64) for c0, c1 in RANGES]
+
+        def join(r, copy, word):
+            c0, c1 = RANGES[r]
+            words = pairs[:, c0 // BLOCK : c1 // BLOCK].rearrange("p b u c e -> p b u (c e)").bitcast(word)
+            copy(
+                out=grouped[r][:].bitcast(word).rearrange("p (b c) u -> p b c u", c=BLOCK),
+                in_=words.rearrange("p b u c -> p b c u"),
+            )
+
+        def quantize_y(r):
+            c0, c1 = RANGES[r]
             nc.vector.quantize_mx(
                 out=y_codes[:, c0:c1].bitcast(FP8X4),
                 scales=y_plane[:, c0:c1],
-                in_=grouped_flat[:, PACK * c0 : PACK * c1],
+                in_=grouped[r][:].rearrange("p c t -> p (c t)"),
             )
+
+        for r in range(4):
+            join(r, nc.scalar.copy, U32)
+        quantize_y(0)
+        join(4, nc.vector.tensor_copy, I32)
+        for r in (1, 4, 2, 3):
+            quantize_y(r)
+
         out_words = out_1[0].rearrange("p c t -> p (c t)").bitcast(I32)
         for c0, c1 in WORD_STORES:
             nc.sync.dma_start(out=out_words[:, c0:c1], in_=y_codes[:, c0:c1].bitcast(I32))

@@ -11,6 +11,7 @@ U8 = mybir.dt.uint8
 FP8X4 = mybir.dt.float8_e4m3fn_x4
 FP4X4 = mybir.dt.float4_e2m1fn_x4
 MULT = mybir.AluOpType.mult
+ADD = mybir.AluOpType.add
 COPY = mybir.ActivationFunctionType.Copy
 
 P = 128
@@ -19,9 +20,14 @@ K, T, N, U = 512, 512, 512, 1024
 FLOPS = 2 * K * N * T
 
 T_GROUPS = ((0, 1), (1, 2), (2, 4))
+SLOT_SLICES = (slice(0, 1), slice(2, 3), slice(1, 4, 2))
+SLOT = (0, 2, 1, 3)
+SHARE = 256
 FIRST = 128
-BLOCK = 128
+BLOCK = 64
+STAGES = ((0, 128), (128, 384), (384, 1024))
 RANGES = ((0, 128), (128, 384), (384, 640), (640, 896), (896, 1024))
+ON_VECTOR = (448, 640)
 WORD_STORES = ((0, 384), (384, 640), (640, 1024))
 
 
@@ -57,6 +63,8 @@ def tile_picked_wroute2_linnone_lo_kernel(
             window = keep.tile([P, U], F32, name=f"window{t}", align_bytes=64)
             nc.vector.memset(window[:].bitcast(I32), 0)
             windows.append(window)
+        shared = keep.tile([P, U], F32, name="window2", align_bytes=64)
+        nc.gpsimd.memset(shared[:].bitcast(I32), 0)
 
         w_grouped = [
             keep.tile([P, t1 - t0, P, PACK], BF16, name=f"w_grouped{t0}", align_bytes=64) for t0, t1 in T_GROUPS
@@ -65,10 +73,9 @@ def tile_picked_wroute2_linnone_lo_kernel(
         w_plane = keep.tile([P, N], U8, name="w_plane", align_bytes=64)
 
         def deal(copy, u, g):
-            t0, t1 = T_GROUPS[g]
             copy(
                 out=w_grouped[g][:, :, :, 2 * u : 2 * u + 2].rearrange("p t m e -> p m t e"),
-                in_=w_raw[u][:].rearrange("p e (m t) -> p m t e", t=PACK)[:, :, t0:t1, :],
+                in_=w_raw[u][:].rearrange("p e (m t) -> p m t e", t=PACK)[:, :, SLOT_SLICES[g], :],
             )
 
         def quantize_w(g):
@@ -88,9 +95,9 @@ def tile_picked_wroute2_linnone_lo_kernel(
         quantize_w(1)
         quantize_w(2)
 
-        def product(t, name, cuts):
+        def product(t, name, cuts, tag=""):
             c0, c1 = cuts[0], cuts[-1]
-            bank = psum.tile([P, T], F32, name=f"bank{name}")
+            bank = psum.tile([P, T], F32, name=f"bank{name}", tag=tag)
             for a, b in zip(cuts, cuts[1:]):
                 nc.tensor.matmul_mx(
                     out=bank[:, a - c0 : b - c0],
@@ -101,16 +108,18 @@ def tile_picked_wroute2_linnone_lo_kernel(
                     start=True,
                     stop=True,
                 )
+            return (bank, c0, c1)
+
+        def gated_product(t, name, cuts, tag=""):
+            bank, c0, c1 = product(t, name, cuts, tag)
             gated = keep.tile([P, c1 - c0], F32, name=f"gated{name}", align_bytes=64)
             nc.vector.tensor_tensor(gated[:], bank[:, 0 : c1 - c0], gates[:, c0:c1], MULT)
             return gated
 
-        head0 = product(0, "0a", (0, FIRST))
-        head1 = product(1, "1a", (0, FIRST))
-        rest0 = product(0, "0b", (FIRST, 2 * FIRST, T))
-        rest1 = product(1, "1b", (FIRST, 2 * FIRST, T))
-        whole2 = product(2, "2", (0, T))
-        whole3 = product(3, "3", (0, T))
+        head0 = gated_product(0, "0a", (0, FIRST))
+        head1 = gated_product(1, "1a", (0, FIRST))
+        rest0 = gated_product(0, "0b", (FIRST, 2 * FIRST, T))
+        whole2 = gated_product(2, "2", (0, T))
 
         out_rows = out_0.rearrange("(p t) c -> p t c", t=PACK)
 
@@ -121,46 +130,49 @@ def tile_picked_wroute2_linnone_lo_kernel(
             nc.vector.tensor_copy(windows[t][:].indirect(offsets[:, c0 // 16 : c1 // 16]), values)
 
         def store(t):
-            nc.sync.dma_start(out=out_rows[:, t, :], in_=windows[t][:])
+            nc.sync.dma_start(out=out_rows[:, SLOT[t], :], in_=windows[t][:])
 
+        window = keep.tile([P, U], F32, name="window3", tag="w_grouped2", align_bytes=64)
+        nc.gpsimd.memset(window[:].bitcast(I32), 0)
+        windows.extend([shared, window])
         on_scalar(0, head0[:], 0, FIRST)
-        for t, tag in ((2, "w_grouped2"), (3, "gated0a")):
-            window = keep.tile([P, U], F32, name=f"window{t}", tag=tag, align_bytes=64)
-            nc.gpsimd.memset(window[:].bitcast(I32), 0)
-            windows.append(window)
         on_scalar(1, head1[:], 0, FIRST)
         on_scalar(0, rest0[:], FIRST, T)
         store(0)
-        on_vector(2, whole2[:, :FIRST], 0, FIRST)
+        on_vector(2, whole2[:, :SHARE], 0, SHARE)
+        on_scalar(2, whole2[:, SHARE:], SHARE, T)
+        store(2)
+        whole3 = gated_product(3, "3", (0, T))
+        rest1 = gated_product(1, "1b", (FIRST, 2 * FIRST, T), tag="bank2")
         on_vector(3, whole3[:], 0, T)
+        store(3)
         on_scalar(1, rest1[:], FIRST, T)
         store(1)
-        store(3)
-        on_scalar(2, whole2[:, FIRST:], FIRST, T)
-        store(2)
 
-        pairs = keep.tile([P, U // BLOCK, 2, BLOCK, 2], BF16, name="pairs", tag="gated3", align_bytes=64)
+        pairs = keep.tile([P, U // BLOCK, 2, BLOCK, 2], BF16, name="pairs", align_bytes=64)
 
-        def stage(t, c0, c1):
-            nc.vector.tensor_copy(
-                out=pairs[:, c0 // BLOCK : c1 // BLOCK, t // 2, :, t % 2],
-                in_=windows[t][:, c0:c1].rearrange("p (b c) -> p b c", c=BLOCK),
+        def views(t, c0, c1):
+            return (
+                pairs[:, c0 // BLOCK : c1 // BLOCK, SLOT[t] // 2, :, SLOT[t] % 2],
+                windows[t][:, c0:c1].rearrange("p (b c) -> p b c", c=BLOCK),
             )
 
-        for t in (0, 3, 1):
-            stage(t, 0, U)
-        for c0, c1 in RANGES:
-            stage(2, c0, c1)
+        for t in (0, 2):
+            staged, values = views(t, 0, U)
+            nc.gpsimd.tensor_scalar(staged, values, 1.0, -0.0, MULT, ADD)
+        nc.vector.tensor_copy(*views(3, 0, U))
+        for c0, c1 in STAGES:
+            nc.vector.tensor_copy(*views(1, c0, c1))
 
         y_codes = keep.tile([P, U], U32, name="y_codes", align_bytes=64)
         y_plane = keep.tile([P, U], U8, name="y_plane", align_bytes=64)
         grouped = [keep.tile([P, c1 - c0, PACK], BF16, name=f"grouped{c0}", align_bytes=64) for c0, c1 in RANGES]
 
-        def join(r, copy, word):
-            c0, c1 = RANGES[r]
+        def join(r, c0, c1, copy, word):
+            first = RANGES[r][0]
             words = pairs[:, c0 // BLOCK : c1 // BLOCK].rearrange("p b u c e -> p b u (c e)").bitcast(word)
             copy(
-                out=grouped[r][:].bitcast(word).rearrange("p (b c) u -> p b c u", c=BLOCK),
+                out=grouped[r][:, c0 - first : c1 - first].bitcast(word).rearrange("p (b c) u -> p b c u", c=BLOCK),
                 in_=words.rearrange("p b u c -> p b c u"),
             )
 
@@ -172,11 +184,12 @@ def tile_picked_wroute2_linnone_lo_kernel(
                 in_=grouped[r][:].rearrange("p c t -> p (c t)"),
             )
 
-        for r in range(4):
-            join(r, nc.scalar.copy, U32)
-        quantize_y(0)
-        join(4, nc.vector.tensor_copy, I32)
-        for r in (1, 4, 2, 3):
+        for r, (c0, c1) in enumerate(RANGES):
+            join(r, c0, ON_VECTOR[0] if r == 2 else c1, nc.scalar.copy, U32)
+            if r == 0:
+                quantize_y(r)
+        join(2, *ON_VECTOR, nc.vector.tensor_copy, I32)
+        for r in range(1, len(RANGES)):
             quantize_y(r)
 
         out_words = out_1[0].rearrange("p c t -> p (c t)").bitcast(I32)

@@ -20,14 +20,13 @@ K, T, N, U = 512, 512, 512, 1024
 FLOPS = 2 * K * N * T
 
 T_GROUPS = ((0, 1), (1, 2), (2, 4))
-SLOT_SLICES = (slice(0, 1), slice(2, 3), slice(1, 4, 2))
-SLOT = (0, 2, 1, 3)
-SHARE = 256
+SHARE = 352
 FIRST = 128
 BLOCK = 64
-STAGES = ((0, 128), (128, 384), (384, 1024))
+OWN = 128
+STAGES = ((3, 128, 384), (2, 128, 384), (3, 384, 1024), (2, 384, 640), (2, 640, 1024))
 RANGES = ((0, 128), (128, 384), (384, 640), (640, 896), (896, 1024))
-ON_VECTOR = (448, 640)
+ON_VECTOR = (512, 640)
 WORD_STORES = ((0, 384), (384, 640), (640, 1024))
 
 
@@ -63,8 +62,6 @@ def tile_picked_wroute2_linnone_lo_kernel(
             window = keep.tile([P, U], F32, name=f"window{t}", align_bytes=64)
             nc.vector.memset(window[:].bitcast(I32), 0)
             windows.append(window)
-        shared = keep.tile([P, U], F32, name="window2", align_bytes=64)
-        nc.gpsimd.memset(shared[:].bitcast(I32), 0)
 
         w_grouped = [
             keep.tile([P, t1 - t0, P, PACK], BF16, name=f"w_grouped{t0}", align_bytes=64) for t0, t1 in T_GROUPS
@@ -73,9 +70,10 @@ def tile_picked_wroute2_linnone_lo_kernel(
         w_plane = keep.tile([P, N], U8, name="w_plane", align_bytes=64)
 
         def deal(copy, u, g):
+            t0, t1 = T_GROUPS[g]
             copy(
                 out=w_grouped[g][:, :, :, 2 * u : 2 * u + 2].rearrange("p t m e -> p m t e"),
-                in_=w_raw[u][:].rearrange("p e (m t) -> p m t e", t=PACK)[:, :, SLOT_SLICES[g], :],
+                in_=w_raw[u][:].rearrange("p e (m t) -> p m t e", t=PACK)[:, :, t0:t1, :],
             )
 
         def quantize_w(g):
@@ -117,9 +115,10 @@ def tile_picked_wroute2_linnone_lo_kernel(
             return gated
 
         head0 = gated_product(0, "0a", (0, FIRST))
-        head1 = gated_product(1, "1a", (0, FIRST))
         rest0 = gated_product(0, "0b", (FIRST, 2 * FIRST, T))
-        whole2 = gated_product(2, "2", (0, T))
+        whole1 = gated_product(1, "1", (0, T))
+        head2 = gated_product(2, "2a", (0, FIRST))
+        whole3 = gated_product(3, "3", (0, T))
 
         out_rows = out_0.rearrange("(p t) c -> p t c", t=PACK)
 
@@ -130,39 +129,40 @@ def tile_picked_wroute2_linnone_lo_kernel(
             nc.vector.tensor_copy(windows[t][:].indirect(offsets[:, c0 // 16 : c1 // 16]), values)
 
         def store(t):
-            nc.sync.dma_start(out=out_rows[:, SLOT[t], :], in_=windows[t][:])
+            nc.sync.dma_start(out=out_rows[:, t, :], in_=windows[t][:])
 
-        window = keep.tile([P, U], F32, name="window3", tag="w_grouped2", align_bytes=64)
-        nc.gpsimd.memset(window[:].bitcast(I32), 0)
-        windows.extend([shared, window])
         on_scalar(0, head0[:], 0, FIRST)
-        on_scalar(1, head1[:], 0, FIRST)
+        for t, tag in ((2, "w_grouped2"), (3, "gated0a")):
+            window = keep.tile([P, U], F32, name=f"window{t}", tag=tag, align_bytes=64)
+            nc.gpsimd.memset(window[:].bitcast(I32), 0)
+            windows.append(window)
         on_scalar(0, rest0[:], FIRST, T)
         store(0)
-        on_vector(2, whole2[:, :SHARE], 0, SHARE)
-        on_scalar(2, whole2[:, SHARE:], SHARE, T)
-        store(2)
-        whole3 = gated_product(3, "3", (0, T))
-        rest1 = gated_product(1, "1b", (FIRST, 2 * FIRST, T), tag="bank2")
+        on_scalar(2, head2[:], 0, FIRST)
+        on_vector(1, whole1[:, :SHARE], 0, SHARE)
+        on_scalar(1, whole1[:, SHARE:], SHARE, T)
+        store(1)
+        rest2 = gated_product(2, "2b", (FIRST, 2 * FIRST, T), tag="bank2a")
         on_vector(3, whole3[:], 0, T)
         store(3)
-        on_scalar(1, rest1[:], FIRST, T)
-        store(1)
+        on_scalar(2, rest2[:], FIRST, T)
+        store(2)
 
         pairs = keep.tile([P, U // BLOCK, 2, BLOCK, 2], BF16, name="pairs", align_bytes=64)
 
         def views(t, c0, c1):
             return (
-                pairs[:, c0 // BLOCK : c1 // BLOCK, SLOT[t] // 2, :, SLOT[t] % 2],
+                pairs[:, c0 // BLOCK : c1 // BLOCK, t // 2, :, t % 2],
                 windows[t][:, c0:c1].rearrange("p (b c) -> p b c", c=BLOCK),
             )
 
-        for t in (0, 2):
+        for t in (0, 1):
             staged, values = views(t, 0, U)
             nc.gpsimd.tensor_scalar(staged, values, 1.0, -0.0, MULT, ADD)
-        nc.vector.tensor_copy(*views(3, 0, U))
-        for c0, c1 in STAGES:
-            nc.vector.tensor_copy(*views(1, c0, c1))
+        for t in (3, 2):
+            nc.scalar.copy(*views(t, 0, OWN))
+        for stage in STAGES:
+            nc.vector.tensor_copy(*views(*stage))
 
         y_codes = keep.tile([P, U], U32, name="y_codes", align_bytes=64)
         y_plane = keep.tile([P, U], U8, name="y_plane", align_bytes=64)

@@ -22,12 +22,12 @@ FLOPS = 2 * K * N * T
 T_GROUPS = ((0, 1), (1, 2), (2, 4))
 SHARE = 352
 FIRST = 128
-BLOCK = 64
-OWN = 128
-STAGES = ((3, 128, 384), (2, 128, 384), (3, 384, 1024), (2, 384, 640), (2, 640, 1024))
-RANGES = ((0, 128), (128, 384), (384, 640), (640, 896), (896, 1024))
-ON_VECTOR = (512, 640)
-WORD_STORES = ((0, 384), (384, 640), (640, 1024))
+BLOCK = 32
+STAGES = ((0, 256), (512, 1024))
+JOINS = ((256, 384), (384, 512), (640, 768), (768, 1024))
+RANGES = ((0, 256), (256, 512), (512, 768), (768, 1024))
+ON_VECTOR = ((0, 256), (512, 640))
+WORD_STORES = ((0, 512), (512, 768), (768, 1024))
 
 
 def tile_picked_wroute2_linnone_lo_kernel(
@@ -159,16 +159,19 @@ def tile_picked_wroute2_linnone_lo_kernel(
         for t in (0, 1):
             staged, values = views(t, 0, U)
             nc.gpsimd.tensor_scalar(staged, values, 1.0, -0.0, MULT, ADD)
-        for t in (3, 2):
-            nc.scalar.copy(*views(t, 0, OWN))
-        for stage in STAGES:
-            nc.vector.tensor_copy(*views(*stage))
+        nc.scalar.copy(*views(3, 256, 512))
+        nc.scalar.copy(*views(2, 256, 384))
+        nc.scalar.copy(*views(2, 384, 512))
+        for c0, c1 in STAGES:
+            nc.vector.tensor_copy(*views(3, c0, c1))
+            nc.vector.tensor_copy(*views(2, c0, c1))
 
         y_codes = keep.tile([P, U], U32, name="y_codes", align_bytes=64)
         y_plane = keep.tile([P, U], U8, name="y_plane", align_bytes=64)
         grouped = [keep.tile([P, c1 - c0, PACK], BF16, name=f"grouped{c0}", align_bytes=64) for c0, c1 in RANGES]
 
-        def join(r, c0, c1, copy, word):
+        def join(c0, c1, copy, word):
+            r = max(i for i, (first, last) in enumerate(RANGES) if first <= c0)
             first = RANGES[r][0]
             words = pairs[:, c0 // BLOCK : c1 // BLOCK].rearrange("p b u c e -> p b u (c e)").bitcast(word)
             copy(
@@ -184,12 +187,11 @@ def tile_picked_wroute2_linnone_lo_kernel(
                 in_=grouped[r][:].rearrange("p c t -> p (c t)"),
             )
 
-        for r, (c0, c1) in enumerate(RANGES):
-            join(r, c0, ON_VECTOR[0] if r == 2 else c1, nc.scalar.copy, U32)
-            if r == 0:
-                quantize_y(r)
-        join(2, *ON_VECTOR, nc.vector.tensor_copy, I32)
-        for r in range(1, len(RANGES)):
+        for c0, c1 in JOINS:
+            join(c0, c1, nc.scalar.copy, U32)
+        for c0, c1 in ON_VECTOR:
+            join(c0, c1, nc.vector.tensor_copy, I32)
+        for r in range(len(RANGES)):
             quantize_y(r)
 
         out_words = out_1[0].rearrange("p c t -> p (c t)").bitcast(I32)

@@ -20,13 +20,13 @@ K, T, N, U = 512, 512, 512, 1024
 FLOPS = 2 * K * N * T
 
 T_GROUPS = ((0, 1), (1, 2), (2, 4))
-SHARE = 352
+SHARE = 320
 FIRST = 128
 BLOCK = 32
 STAGES = ((0, 256), (512, 1024))
-JOINS = ((256, 384), (384, 512), (640, 768), (768, 1024))
+JOINS = ((256, 384), (384, 512), (768, 1024))
 RANGES = ((0, 256), (256, 512), (512, 768), (768, 1024))
-ON_VECTOR = ((0, 256), (512, 640))
+ON_VECTOR = ((0, 256), (512, 768))
 WORD_STORES = ((0, 512), (512, 768), (768, 1024))
 
 

@@ -22,7 +22,6 @@ FLOPS = 2 * K * N * T
 T_GROUPS = ((0, 1), (1, 2), (2, 4))
 SHARE = 320
 FIRST = 128
-BLOCK = 32
 STAGES = ((0, 256), (512, 1024))
 JOINS = ((256, 384), (384, 512), (768, 1024))
 RANGES = ((0, 256), (256, 512), (512, 768), (768, 1024))
@@ -148,13 +147,10 @@ def tile_picked_wroute2_linnone_lo_kernel(
         on_scalar(2, rest2[:], FIRST, T)
         store(2)
 
-        pairs = keep.tile([P, U // BLOCK, 2, BLOCK, 2], BF16, name="pairs", align_bytes=64)
+        pairs = keep.tile([P, 2, U, 2], BF16, name="pairs", align_bytes=64)
 
         def views(t, c0, c1):
-            return (
-                pairs[:, c0 // BLOCK : c1 // BLOCK, t // 2, :, t % 2],
-                windows[t][:, c0:c1].rearrange("p (b c) -> p b c", c=BLOCK),
-            )
+            return (pairs[:, t // 2, c0:c1, t % 2], windows[t][:, c0:c1])
 
         for t in (0, 1):
             staged, values = views(t, 0, U)
@@ -173,11 +169,8 @@ def tile_picked_wroute2_linnone_lo_kernel(
         def join(c0, c1, copy, word):
             r = max(i for i, (first, last) in enumerate(RANGES) if first <= c0)
             first = RANGES[r][0]
-            words = pairs[:, c0 // BLOCK : c1 // BLOCK].rearrange("p b u c e -> p b u (c e)").bitcast(word)
-            copy(
-                out=grouped[r][:, c0 - first : c1 - first].bitcast(word).rearrange("p (b c) u -> p b c u", c=BLOCK),
-                in_=words.rearrange("p b u c -> p b c u"),
-            )
+            words = pairs[:, :, c0:c1, :].rearrange("p u c e -> p u (c e)").bitcast(word)
+            copy(out=grouped[r][:, c0 - first : c1 - first].bitcast(word), in_=words.rearrange("p u c -> p c u"))
 
         def quantize_y(r):
             c0, c1 = RANGES[r]

@@ -20,7 +20,7 @@ K, T, N, U = 512, 512, 512, 1024
 FLOPS = 2 * K * N * T
 
 T_GROUPS = ((0, 1), (1, 2), (2, 4))
-SHARE = 320
+SHARE = 192
 FIRST = 128
 STAGES = ((0, 256), (512, 1024))
 JOINS = ((256, 384), (384, 512), (768, 1024))
@@ -56,11 +56,10 @@ def tile_picked_wroute2_linnone_lo_kernel(
         nc.sync.dma_start(out=x_codes[:].bitcast(I32), in_=x_words[0].bitcast(I32))
         nc.sync.dma_start(out=gates[:], in_=gate)
 
-        windows = []
-        for t in range(2):
-            window = keep.tile([P, U], F32, name=f"window{t}", align_bytes=64)
-            nc.vector.memset(window[:].bitcast(I32), 0)
-            windows.append(window)
+        windows = {}
+        for t in (0, 1, 3):
+            windows[t] = keep.tile([P, U], F32, name=f"window{t}", align_bytes=64)
+            nc.vector.memset(windows[t][:].bitcast(I32), 0)
 
         w_grouped = [
             keep.tile([P, t1 - t0, P, PACK], BF16, name=f"w_grouped{t0}", align_bytes=64) for t0, t1 in T_GROUPS
@@ -83,11 +82,10 @@ def tile_picked_wroute2_linnone_lo_kernel(
                 in_=w_grouped[g][:].rearrange("p t m j -> p (t m j)"),
             )
 
-        for g in range(3):
-            deal(nc.vector.tensor_copy, 0, g)
-        deal(nc.vector.tensor_copy, 1, 0)
-        deal(nc.vector.tensor_copy, 1, 1)
-        deal(nc.scalar.copy, 1, 2)
+        for u in range(2):
+            deal(nc.vector.tensor_copy, u, 0)
+            deal(nc.vector.tensor_copy, u, 1)
+            deal(nc.scalar.copy, u, 2)
         quantize_w(0)
         quantize_w(1)
         quantize_w(2)
@@ -116,8 +114,7 @@ def tile_picked_wroute2_linnone_lo_kernel(
         head0 = gated_product(0, "0a", (0, FIRST))
         rest0 = gated_product(0, "0b", (FIRST, 2 * FIRST, T))
         whole1 = gated_product(1, "1", (0, T))
-        head2 = gated_product(2, "2a", (0, FIRST))
-        whole3 = gated_product(3, "3", (0, T))
+        whole2 = gated_product(2, "2", (0, T))
 
         out_rows = out_0.rearrange("(p t) c -> p t c", t=PACK)
 
@@ -131,20 +128,18 @@ def tile_picked_wroute2_linnone_lo_kernel(
             nc.sync.dma_start(out=out_rows[:, t, :], in_=windows[t][:])
 
         on_scalar(0, head0[:], 0, FIRST)
-        for t, tag in ((2, "w_grouped2"), (3, "gated0a")):
-            window = keep.tile([P, U], F32, name=f"window{t}", tag=tag, align_bytes=64)
-            nc.gpsimd.memset(window[:].bitcast(I32), 0)
-            windows.append(window)
+        windows[2] = keep.tile([P, U], F32, name="window2", tag="w_grouped2", align_bytes=64)
+        nc.gpsimd.memset(windows[2][:].bitcast(I32), 0)
         on_scalar(0, rest0[:], FIRST, T)
         store(0)
-        on_scalar(2, head2[:], 0, FIRST)
         on_vector(1, whole1[:, :SHARE], 0, SHARE)
         on_scalar(1, whole1[:, SHARE:], SHARE, T)
         store(1)
-        rest2 = gated_product(2, "2b", (FIRST, 2 * FIRST, T), tag="bank2a")
+        whole3 = gated_product(3, "3", (0, T))
+        on_vector(2, whole2[:, :FIRST], 0, FIRST)
         on_vector(3, whole3[:], 0, T)
         store(3)
-        on_scalar(2, rest2[:], FIRST, T)
+        on_scalar(2, whole2[:, FIRST:], FIRST, T)
         store(2)
 
         pairs = keep.tile([P, 2, U, 2], BF16, name="pairs", align_bytes=64)

@@ -20,8 +20,9 @@ K, T, N, U = 512, 512, 512, 1024
 FLOPS = 2 * K * N * T
 
 T_GROUPS = ((0, 1), (1, 2), (2, 4))
-SHARE = 192
+SHARE = 224
 FIRST = 128
+HALF = 256
 STAGES = ((0, 256), (512, 1024))
 JOINS = ((256, 384), (384, 512), (768, 1024))
 RANGES = ((0, 256), (256, 512), (512, 768), (768, 1024))
@@ -90,56 +91,52 @@ def tile_picked_wroute2_linnone_lo_kernel(
         quantize_w(1)
         quantize_w(2)
 
-        def product(t, name, cuts, tag=""):
-            c0, c1 = cuts[0], cuts[-1]
-            bank = psum.tile([P, T], F32, name=f"bank{name}", tag=tag)
-            for a, b in zip(cuts, cuts[1:]):
-                nc.tensor.matmul_mx(
-                    out=bank[:, a - c0 : b - c0],
-                    lhsT=w_codes[:, t * P : (t + 1) * P].bitcast(FP8X4),
-                    lhsT_scale=w_plane[:, t * P : (t + 1) * P],
-                    rhs=x_codes[:, 2 * a : 2 * b].bitcast(FP4X4),
-                    rhs_scale=x_plane[:, a:b],
-                    start=True,
-                    stop=True,
-                )
-            return (bank, c0, c1)
+        gated = [keep.tile([P, T], F32, name=f"gated{t}", align_bytes=64) for t in range(PACK)]
 
-        def gated_product(t, name, cuts, tag=""):
-            bank, c0, c1 = product(t, name, cuts, tag)
-            gated = keep.tile([P, c1 - c0], F32, name=f"gated{name}", align_bytes=64)
-            nc.vector.tensor_tensor(gated[:], bank[:, 0 : c1 - c0], gates[:, c0:c1], MULT)
-            return gated
+        def gated_product(t, c0, c1):
+            bank = psum.tile([P, T], F32, name=f"bank{t}_{c0}")
+            nc.tensor.matmul_mx(
+                out=bank[:, 0 : c1 - c0],
+                lhsT=w_codes[:, t * P : (t + 1) * P].bitcast(FP8X4),
+                lhsT_scale=w_plane[:, t * P : (t + 1) * P],
+                rhs=x_codes[:, 2 * c0 : 2 * c1].bitcast(FP4X4),
+                rhs_scale=x_plane[:, c0:c1],
+                start=True,
+                stop=True,
+            )
+            nc.vector.tensor_tensor(gated[t][:, c0:c1], bank[:, 0 : c1 - c0], gates[:, c0:c1], MULT)
 
-        head0 = gated_product(0, "0a", (0, FIRST))
-        rest0 = gated_product(0, "0b", (FIRST, 2 * FIRST, T))
-        whole1 = gated_product(1, "1", (0, T))
-        whole2 = gated_product(2, "2", (0, T))
+        gated_product(0, 0, FIRST)
+        gated_product(0, FIRST, HALF)
+        gated_product(0, HALF, T)
+        gated_product(1, 0, HALF)
+        gated_product(1, HALF, T)
 
         out_rows = out_0.rearrange("(p t) c -> p t c", t=PACK)
 
-        def on_scalar(t, values, c0, c1):
-            nc.scalar.activation(windows[t][:].indirect(offsets[:, c0 // 16 : c1 // 16]), values, COPY)
+        def on_scalar(t, c0, c1):
+            nc.scalar.activation(windows[t][:].indirect(offsets[:, c0 // 16 : c1 // 16]), gated[t][:, c0:c1], COPY)
 
-        def on_vector(t, values, c0, c1):
-            nc.vector.tensor_copy(windows[t][:].indirect(offsets[:, c0 // 16 : c1 // 16]), values)
+        def on_vector(t, c0, c1):
+            nc.vector.tensor_copy(windows[t][:].indirect(offsets[:, c0 // 16 : c1 // 16]), gated[t][:, c0:c1])
 
         def store(t):
             nc.sync.dma_start(out=out_rows[:, t, :], in_=windows[t][:])
 
-        on_scalar(0, head0[:], 0, FIRST)
+        on_scalar(0, 0, FIRST)
         windows[2] = keep.tile([P, U], F32, name="window2", tag="w_grouped2", align_bytes=64)
         nc.gpsimd.memset(windows[2][:].bitcast(I32), 0)
-        on_scalar(0, rest0[:], FIRST, T)
+        on_scalar(0, FIRST, T)
         store(0)
-        on_vector(1, whole1[:, :SHARE], 0, SHARE)
-        on_scalar(1, whole1[:, SHARE:], SHARE, T)
+        on_vector(1, 0, SHARE)
+        on_scalar(1, SHARE, T)
         store(1)
-        whole3 = gated_product(3, "3", (0, T))
-        on_vector(2, whole2[:, :FIRST], 0, FIRST)
-        on_vector(3, whole3[:], 0, T)
+        gated_product(2, 0, T)
+        gated_product(3, 0, T)
+        on_vector(2, 0, FIRST)
+        on_vector(3, 0, T)
         store(3)
-        on_scalar(2, whole2[:, FIRST:], FIRST, T)
+        on_scalar(2, FIRST, T)
         store(2)
 
         pairs = keep.tile([P, 2, U, 2], BF16, name="pairs", align_bytes=64)

@@ -25,9 +25,9 @@ FIRST = 128
 HALF = 256
 STAGES = ((0, 256), (512, 1024))
 JOINS = ((256, 384), (384, 512), (768, 1024))
-RANGES = ((0, 256), (256, 512), (512, 768), (768, 1024))
+RANGES = ((0, 256), (256, 384), (384, 768), (768, 1024))
 ON_VECTOR = ((0, 256), (512, 768))
-WORD_STORES = ((0, 512), (512, 768), (768, 1024))
+WORD_STORES = ((0, 384), (384, 768), (768, 1024))
 
 
 def tile_picked_wroute2_linnone_lo_kernel(

@@ -20,7 +20,7 @@ K, T, N, U = 512, 512, 512, 1024
 FLOPS = 2 * K * N * T
 
 T_GROUPS = ((0, 1), (1, 2), (2, 4))
-SHARE = 224
+SHARE = 352
 FIRST = 128
 HALF = 256
 STAGES = ((0, 256), (512, 1024))
@@ -57,6 +57,8 @@ def tile_picked_wroute2_linnone_lo_kernel(
         nc.sync.dma_start(out=x_codes[:].bitcast(I32), in_=x_words[0].bitcast(I32))
         nc.sync.dma_start(out=gates[:], in_=gate)
 
+        unit = keep.tile([P, 1], F32, name="unit")
+        nc.vector.memset(unit[:], 1.0)
         windows = {}
         for t in (0, 1, 3):
             windows[t] = keep.tile([P, U], F32, name=f"window{t}", align_bytes=64)
@@ -93,29 +95,35 @@ def tile_picked_wroute2_linnone_lo_kernel(
 
         gated = [keep.tile([P, T], F32, name=f"gated{t}", align_bytes=64) for t in range(PACK)]
 
-        def gated_product(t, c0, c1):
-            bank = psum.tile([P, T], F32, name=f"bank{t}_{c0}")
-            nc.tensor.matmul_mx(
-                out=bank[:, 0 : c1 - c0],
-                lhsT=w_codes[:, t * P : (t + 1) * P].bitcast(FP8X4),
-                lhsT_scale=w_plane[:, t * P : (t + 1) * P],
-                rhs=x_codes[:, 2 * c0 : 2 * c1].bitcast(FP4X4),
-                rhs_scale=x_plane[:, c0:c1],
-                start=True,
-                stop=True,
-            )
-            nc.vector.tensor_tensor(gated[t][:, c0:c1], bank[:, 0 : c1 - c0], gates[:, c0:c1], MULT)
+        def product(t, cuts, tag=""):
+            c0, c1 = cuts[0], cuts[-1]
+            bank = psum.tile([P, T], F32, name=f"bank{t}_{c0}", tag=tag)
+            for a, b in zip(cuts, cuts[1:]):
+                nc.tensor.matmul_mx(
+                    out=bank[:, a - c0 : b - c0],
+                    lhsT=w_codes[:, t * P : (t + 1) * P].bitcast(FP8X4),
+                    lhsT_scale=w_plane[:, t * P : (t + 1) * P],
+                    rhs=x_codes[:, 2 * a : 2 * b].bitcast(FP4X4),
+                    rhs_scale=x_plane[:, a:b],
+                    start=True,
+                    stop=True,
+                )
+            return bank[:, 0 : c1 - c0]
 
-        gated_product(0, 0, FIRST)
-        gated_product(0, FIRST, HALF)
-        gated_product(0, HALF, T)
-        gated_product(1, 0, HALF)
-        gated_product(1, HALF, T)
+        def gated_product(t, *cuts, tag=""):
+            c0, c1 = cuts[0], cuts[-1]
+            nc.vector.tensor_tensor(gated[t][:, c0:c1], product(t, cuts, tag), gates[:, c0:c1], MULT)
+
+        gated_product(0, 0, FIRST, tag="first")
+        gated_product(0, FIRST, HALF, tag="second")
+        gated_product(1, FIRST, T - FIRST, tag="third")
+        gated_product(0, HALF, T, tag="fourth")
+        gated_product(1, T - FIRST, T, tag="fifth")
 
         out_rows = out_0.rearrange("(p t) c -> p t c", t=PACK)
 
         def on_scalar(t, c0, c1):
-            nc.scalar.activation(windows[t][:].indirect(offsets[:, c0 // 16 : c1 // 16]), gated[t][:, c0:c1], COPY)
+            nc.scalar.activation(windows[t][:].indirect(offsets[:, c0 // 16 : c1 // 16]), gated[t][:, c0:c1], COPY, scale=unit[:])
 
         def on_vector(t, c0, c1):
             nc.vector.tensor_copy(windows[t][:].indirect(offsets[:, c0 // 16 : c1 // 16]), gated[t][:, c0:c1])
@@ -126,17 +134,20 @@ def tile_picked_wroute2_linnone_lo_kernel(
         on_scalar(0, 0, FIRST)
         windows[2] = keep.tile([P, U], F32, name="window2", tag="w_grouped2", align_bytes=64)
         nc.gpsimd.memset(windows[2][:].bitcast(I32), 0)
+        plain = keep.tile([P, FIRST], F32, name="plain", align_bytes=64)
+        nc.scalar.copy(plain[:], product(1, (0, FIRST), "first"))
         on_scalar(0, FIRST, T)
         store(0)
-        on_vector(1, 0, SHARE)
+        on_vector(1, FIRST, SHARE)
+        gated_product(3, 0, HALF, tag="second")
+        nc.vector.tensor_tensor(windows[1][:].indirect(offsets[:, 0 : FIRST // 16]), plain[:], gates[:, 0:FIRST], MULT)
         on_scalar(1, SHARE, T)
         store(1)
-        gated_product(2, 0, T)
-        gated_product(3, 0, T)
-        on_vector(2, 0, FIRST)
+        gated_product(3, HALF, T, tag="third")
+        gated_product(2, 0, T, tag="fourth")
         on_vector(3, 0, T)
         store(3)
-        on_scalar(2, FIRST, T)
+        on_scalar(2, 0, T)
         store(2)
 
         pairs = keep.tile([P, 2, U, 2], BF16, name="pairs", align_bytes=64)

@@ -20,7 +20,7 @@ K, T, N, U = 512, 512, 512, 1024
 FLOPS = 2 * K * N * T
 
 T_GROUPS = ((0, 1), (1, 2), (2, 4))
-SHARE = 352
+SHARE = 384
 FIRST = 128
 HALF = 256
 STAGES = ((0, 256), (512, 1024))
@@ -116,9 +116,8 @@ def tile_picked_wroute2_linnone_lo_kernel(
 
         gated_product(0, 0, FIRST, tag="first")
         gated_product(0, FIRST, HALF, tag="second")
-        gated_product(1, FIRST, T - FIRST, tag="third")
+        gated_product(1, HALF, T, tag="third")
         gated_product(0, HALF, T, tag="fourth")
-        gated_product(1, T - FIRST, T, tag="fifth")
 
         out_rows = out_0.rearrange("(p t) c -> p t c", t=PACK)
 
@@ -134,13 +133,13 @@ def tile_picked_wroute2_linnone_lo_kernel(
         on_scalar(0, 0, FIRST)
         windows[2] = keep.tile([P, U], F32, name="window2", tag="w_grouped2", align_bytes=64)
         nc.gpsimd.memset(windows[2][:].bitcast(I32), 0)
-        plain = keep.tile([P, FIRST], F32, name="plain", align_bytes=64)
-        nc.scalar.copy(plain[:], product(1, (0, FIRST), "first"))
+        plain = keep.tile([P, HALF], F32, name="plain", align_bytes=64)
+        nc.scalar.copy(plain[:], product(1, (0, HALF), "first"))
         on_scalar(0, FIRST, T)
         store(0)
-        on_vector(1, FIRST, SHARE)
+        on_vector(1, HALF, SHARE)
         gated_product(3, 0, HALF, tag="second")
-        nc.vector.tensor_tensor(windows[1][:].indirect(offsets[:, 0 : FIRST // 16]), plain[:], gates[:, 0:FIRST], MULT)
+        nc.vector.tensor_tensor(windows[1][:].indirect(offsets[:, 0 : HALF // 16]), plain[:], gates[:, 0:HALF], MULT)
         on_scalar(1, SHARE, T)
         store(1)
         gated_product(3, HALF, T, tag="third")

@@ -116,7 +116,7 @@ def tile_picked_wroute2_linnone_lo_kernel(
 
         gated_product(0, 0, FIRST, tag="first")
         gated_product(0, FIRST, HALF, tag="second")
-        gated_product(1, HALF, T, tag="third")
+        gated_product(1, HALF, SHARE, tag="third")
         gated_product(0, HALF, T, tag="fourth")
 
         out_rows = out_0.rearrange("(p t) c -> p t c", t=PACK)
@@ -139,11 +139,12 @@ def tile_picked_wroute2_linnone_lo_kernel(
         store(0)
         on_vector(1, HALF, SHARE)
         gated_product(3, 0, HALF, tag="second")
+        gated_product(1, SHARE, T, tag="third")
         nc.vector.tensor_tensor(windows[1][:].indirect(offsets[:, 0 : HALF // 16]), plain[:], gates[:, 0:HALF], MULT)
         on_scalar(1, SHARE, T)
         store(1)
-        gated_product(3, HALF, T, tag="third")
-        gated_product(2, 0, T, tag="fourth")
+        gated_product(3, HALF, T, tag="fourth")
+        gated_product(2, 0, T, tag="second")
         on_vector(3, 0, T)
         store(3)
         on_scalar(2, 0, T)

@@ -117,7 +117,8 @@ def tile_picked_wroute2_linnone_lo_kernel(
         gated_product(0, 0, FIRST, tag="first")
         gated_product(0, FIRST, HALF, tag="second")
         gated_product(1, HALF, SHARE, tag="third")
-        gated_product(0, HALF, T, tag="fourth")
+        gated_product(0, HALF, SHARE, tag="fourth")
+        gated_product(0, SHARE, T, tag="fifth")
 
         out_rows = out_0.rearrange("(p t) c -> p t c", t=PACK)
 
@@ -143,7 +144,7 @@ def tile_picked_wroute2_linnone_lo_kernel(
         nc.vector.tensor_tensor(windows[1][:].indirect(offsets[:, 0 : HALF // 16]), plain[:], gates[:, 0:HALF], MULT)
         on_scalar(1, SHARE, T)
         store(1)
-        gated_product(3, HALF, T, tag="fourth")
+        gated_product(3, HALF, T, tag="fifth")
         gated_product(2, 0, T, tag="second")
         on_vector(3, 0, T)
         store(3)

from contextlib import ExitStack

import concourse.mybir as mybir

F32 = mybir.dt.float32
BF16 = mybir.dt.bfloat16
I32 = mybir.dt.int32
U32 = mybir.dt.uint32
U16 = mybir.dt.uint16
U8 = mybir.dt.uint8
FP8X4 = mybir.dt.float8_e4m3fn_x4
FP4X4 = mybir.dt.float4_e2m1fn_x4
MULT = mybir.AluOpType.mult
ADD = mybir.AluOpType.add
COPY = mybir.ActivationFunctionType.Copy

P = 128
PACK = 4
K, T, N, U = 512, 512, 512, 1024
FLOPS = 2 * K * N * T

T_GROUPS = ((0, 1), (1, 2), (2, 4))
SHARE = 384
FIRST = 128
HALF = 256
STAGES = ((0, 256), (512, 1024))
JOINS = ((256, 384), (384, 512), (768, 1024))
RANGES = ((0, 256), (256, 384), (384, 768), (768, 1024))
ON_VECTOR = ((0, 256), (512, 768))
WORD_STORES = ((0, 384), (384, 768), (768, 1024))


def tile_picked_wroute2_linnone_lo_kernel(
    tc, x_words, x_scales, gate, w1, dst, out_0, out_1, out_2
):
    nc = tc.nc
    with ExitStack() as ctx:
        keep = ctx.enter_context(tc.tile_pool(name="keep", bufs=1))
        psum = ctx.enter_context(tc.psum_pool(name="psum", bufs=1))

        w_pairs = w1.rearrange("(p u e) c -> p u e c", u=2, e=2)
        w_raw = [keep.tile([P, 2, N], F32, name=f"w_raw{u}", align_bytes=64) for u in range(2)]
        offsets = keep.tile([P, T // 16], U16, name="offsets")
        x_plane = keep.tile([P, T], U8, name="x_plane", align_bytes=64)
        x_codes = keep.tile([P, 2 * T], U8, name="x_codes", align_bytes=64)
        gates = keep.tile([P, T], F32, name="gates", align_bytes=64)

        nc.vector.memset(x_plane[:].bitcast(I32), 0)
        nc.sync.dma_start(out=w_raw[0][:], in_=w_pairs[:, 0, :, :])
        nc.sync.dma_start(out=w_raw[1][:], in_=w_pairs[:, 1, :, :])
        nc.sync.dma_start(offsets[:], dst)
        for q in range(4):
            nc.sync.dma_start(
                out=x_plane[32 * q : 32 * q + 4, :].bitcast(I32),
                in_=x_scales[0, 4 * q : 4 * q + 4, :].bitcast(I32),
            )
        nc.sync.dma_start(out=x_codes[:].bitcast(I32), in_=x_words[0].bitcast(I32))
        nc.sync.dma_start(out=gates[:], in_=gate)

        unit = keep.tile([P, 1], F32, name="unit")
        nc.vector.memset(unit[:], 1.0)
        windows = {}
        for t in (0, 1, 3):
            windows[t] = keep.tile([P, U], F32, name=f"window{t}", align_bytes=64)
            nc.vector.memset(windows[t][:].bitcast(I32), 0)

        w_grouped = [
            keep.tile([P, t1 - t0, P, PACK], BF16, name=f"w_grouped{t0}", align_bytes=64) for t0, t1 in T_GROUPS
        ]
        w_codes = keep.tile([P, N], U32, name="w_codes", align_bytes=64)
        w_plane = keep.tile([P, N], U8, name="w_plane", align_bytes=64)

        def deal(copy, u, g):
            t0, t1 = T_GROUPS[g]
            copy(
                out=w_grouped[g][:, :, :, 2 * u : 2 * u + 2].rearrange("p t m e -> p m t e"),
                in_=w_raw[u][:].rearrange("p e (m t) -> p m t e", t=PACK)[:, :, t0:t1, :],
            )

        def quantize_w(g):
            t0, t1 = T_GROUPS[g]
            nc.vector.quantize_mx(
                out=w_codes[:, t0 * P : t1 * P].bitcast(FP8X4),
                scales=w_plane[:, t0 * P : t1 * P],
                in_=w_grouped[g][:].rearrange("p t m j -> p (t m j)"),
            )

        for u in range(2):
            deal(nc.vector.tensor_copy, u, 0)
            deal(nc.vector.tensor_copy, u, 1)
            deal(nc.scalar.copy, u, 2)
        quantize_w(0)
        quantize_w(1)
        quantize_w(2)

        gated = [keep.tile([P, T], F32, name=f"gated{t}", align_bytes=64) for t in range(PACK)]

        def product(t, cuts, tag=""):
            c0, c1 = cuts[0], cuts[-1]
            bank = psum.tile([P, T], F32, name=f"bank{t}_{c0}", tag=tag)
            for a, b in zip(cuts, cuts[1:]):
                nc.tensor.matmul_mx(
                    out=bank[:, a - c0 : b - c0],
                    lhsT=w_codes[:, t * P : (t + 1) * P].bitcast(FP8X4),
                    lhsT_scale=w_plane[:, t * P : (t + 1) * P],
                    rhs=x_codes[:, 2 * a : 2 * b].bitcast(FP4X4),
                    rhs_scale=x_plane[:, a:b],
                    start=True,
                    stop=True,
                )
            return bank[:, 0 : c1 - c0]

        def gated_product(t, *cuts, tag=""):
            c0, c1 = cuts[0], cuts[-1]
            nc.vector.tensor_tensor(gated[t][:, c0:c1], product(t, cuts, tag), gates[:, c0:c1], MULT)

        gated_product(0, 0, FIRST, tag="first")
        gated_product(0, FIRST, HALF, tag="second")
        gated_product(1, HALF, SHARE, tag="third")
        gated_product(0, HALF, SHARE, tag="fourth")
        gated_product(0, SHARE, T, tag="fifth")

        out_rows = out_0.rearrange("(p t) c -> p t c", t=PACK)

        def on_scalar(t, c0, c1):
            nc.scalar.activation(windows[t][:].indirect(offsets[:, c0 // 16 : c1 // 16]), gated[t][:, c0:c1], COPY, scale=unit[:])

        def on_vector(t, c0, c1):
            nc.vector.tensor_copy(windows[t][:].indirect(offsets[:, c0 // 16 : c1 // 16]), gated[t][:, c0:c1])

        def store(t):
            nc.sync.dma_start(out=out_rows[:, t, :], in_=windows[t][:])

        on_scalar(0, 0, FIRST)
        windows[2] = keep.tile([P, U], F32, name="window2", tag="w_grouped2", align_bytes=64)
        nc.gpsimd.memset(windows[2][:].bitcast(I32), 0)
        plain = keep.tile([P, HALF], F32, name="plain", align_bytes=64)
        nc.scalar.copy(plain[:], product(1, (0, HALF), "first"))
        on_scalar(0, FIRST, T)
        store(0)
        on_vector(1, HALF, SHARE)
        gated_product(3, 0, HALF, tag="second")
        gated_product(1, SHARE, T, tag="third")
        nc.vector.tensor_tensor(windows[1][:].indirect(offsets[:, 0 : HALF // 16]), plain[:], gates[:, 0:HALF], MULT)
        on_scalar(1, SHARE, T)
        store(1)
        gated_product(3, HALF, T, tag="fifth")
        gated_product(2, 0, T, tag="second")
        on_vector(3, 0, T)
        store(3)
        on_scalar(2, 0, T)
        store(2)

        pairs = keep.tile([P, 2, U, 2], BF16, name="pairs", align_bytes=64)

        def views(t, c0, c1):
            return (pairs[:, t // 2, c0:c1, t % 2], windows[t][:, c0:c1])

        for t in (0, 1):
            staged, values = views(t, 0, U)
            nc.gpsimd.tensor_scalar(staged, values, 1.0, -0.0, MULT, ADD)
        nc.scalar.copy(*views(3, 256, 512))
        nc.scalar.copy(*views(2, 256, 384))
        nc.scalar.copy(*views(2, 384, 512))
        for c0, c1 in STAGES:
            nc.vector.tensor_copy(*views(3, c0, c1))
            nc.vector.tensor_copy(*views(2, c0, c1))

        y_codes = keep.tile([P, U], U32, name="y_codes", align_bytes=64)
        y_plane = keep.tile([P, U], U8, name="y_plane", align_bytes=64)
        grouped = [keep.tile([P, c1 - c0, PACK], BF16, name=f"grouped{c0}", align_bytes=64) for c0, c1 in RANGES]

        def join(c0, c1, copy, word):
            r = max(i for i, (first, last) in enumerate(RANGES) if first <= c0)
            first = RANGES[r][0]
            words = pairs[:, :, c0:c1, :].rearrange("p u c e -> p u (c e)").bitcast(word)
            copy(out=grouped[r][:, c0 - first : c1 - first].bitcast(word), in_=words.rearrange("p u c -> p c u"))

        def quantize_y(r):
            c0, c1 = RANGES[r]
            nc.vector.quantize_mx(
                out=y_codes[:, c0:c1].bitcast(FP8X4),
                scales=y_plane[:, c0:c1],
                in_=grouped[r][:].rearrange("p c t -> p (c t)"),
            )

        for c0, c1 in JOINS:
            join(c0, c1, nc.scalar.copy, U32)
        for c0, c1 in ON_VECTOR:
            join(c0, c1, nc.vector.tensor_copy, I32)
        for r in range(len(RANGES)):
            quantize_y(r)

        out_words = out_1[0].rearrange("p c t -> p (c t)").bitcast(I32)
        for c0, c1 in WORD_STORES:
            nc.sync.dma_start(out=out_words[:, c0:c1], in_=y_codes[:, c0:c1].bitcast(I32))
        for q in range(4):
            queue = nc.scalar if q < 3 else nc.sync
            queue.dma_start(
                out=out_2[0, 4 * q : 4 * q + 4, :].bitcast(I32),
                in_=y_plane[32 * q : 32 * q + 4, :].bitcast(I32),
            )
